import numpy as np
import ml_dtypes


def mxq(x, axis, fmt="e4m3"):
    dtype, down = {"e4m3": (ml_dtypes.float8_e4m3fn, 7), "e5m2": (ml_dtypes.float8_e5m2, 14)}[fmt]
    v = np.moveaxis(np.asarray(x, np.float32).astype(ml_dtypes.bfloat16).astype(np.float64), axis, -1)
    blocks = v.reshape(v.shape[:-1] + (-1, 32))
    amax = np.abs(blocks).max(-1, keepdims=True)
    byte = np.maximum(np.where(amax > 0, np.frexp(amax)[1] - 1 + 127, 0) - down, 1)
    scale = np.exp2(byte - 127.0)
    codes = (blocks / scale).astype(np.float32).astype(dtype).astype(np.float64)
    return np.moveaxis((codes * scale).reshape(v.shape), -1, axis)


WIDE = False


def mx_kscale(k):
    if not WIDE:
        return np.ones(k)
    levels = np.array([10, -10, 5, -5, 0])
    if k % 512:
        return np.exp2(np.random.permutation(np.resize(levels, k // 32))).repeat(32)
    a = np.empty((k // 512, 16))
    for p in range(k // 512):
        a[p, :8] = np.random.permutation(np.resize(levels, 8))
        for g in range(8):
            far = levels[np.abs(levels - a[p, g]) >= 10]
            a[p, g + 8] = far[np.random.randint(len(far))]
    return np.exp2(a.ravel()).repeat(32)


def f64(x):
    return np.asarray(x).astype(np.float64)


def striped(idx):
    return np.tile(idx.reshape(-1, 16).T, (8, 1)).astype(np.uint16)


def unstriped(offs):
    return offs[:16].T.reshape(-1).astype(np.int64)


E2M1 = np.array([0.0, 0.5, 1.0, 1.5, 2.0, 3.0, 4.0, 6.0, -0.0, -0.5, -1.0, -1.5, -2.0, -3.0, -4.0, -6.0])


def pack_fp4(w):
    k, n = w.shape
    w = f64(np.asarray(w, np.float32).astype(ml_dtypes.bfloat16)).reshape(k // 32, 32, n)
    amax = np.abs(w).max(1)
    mant, ex = np.frexp(amax / 6.0)
    byte = np.clip(np.where(amax > 0, np.where(mant > 0.5, ex, ex - 1) + 127, 1), 1, 254)
    scaled = (w * np.exp2(127.0 - byte)[:, None, :]).reshape(k, n).astype(np.float32)
    c = np.ascontiguousarray(scaled.reshape(k // 512, 128, 4, n).transpose(0, 1, 3, 2)).astype(ml_dtypes.float4_e2m1fn).view(np.uint8) & 0xF
    words = (c[..., 0::2] | (c[..., 1::2] << 4)).reshape(k // 512, 128, 2 * n)
    return np.ascontiguousarray(words), np.ascontiguousarray(byte.astype(np.uint8).reshape(k // 512, 16, n))


def unpack_fp4(words, scales):
    g, _, n = scales.shape
    words = np.ascontiguousarray(words).reshape(g, 128, n, 2)
    nib = np.empty((g, 128, n, 4), np.uint8)
    nib[..., 0::2] = words & 0xF
    nib[..., 1::2] = words >> 4
    vals = E2M1[nib] * np.repeat(np.exp2(scales.astype(np.float64) - 127.0), 8, axis=1)[..., None]
    return vals.transpose(0, 1, 3, 2).reshape(g * 512, n)


def relu(v):
    return np.maximum(v, 0.0)


K, T, S, H, N = 512, 1024, 512, 512, 128


def setup_inputs():
    n = np.random.standard_normal
    s = mx_kscale(K)[:, None]
    u = mx_kscale(H)
    packed_xT = pack_fp4(n((K, T)) * s)
    return {
        "x_words": packed_xT[0],
        "x_scales": packed_xT[1],
        "w1": (n((K, H)) / np.sqrt(K) / s).astype(np.float32),
        "w2": (n((H, N)) / np.sqrt(H) / u[:, None]).astype(np.float32),
        "gamma": (np.random.uniform(0.5, 1.5, (H, 1)) * u[:, None]).astype(np.float32),
        "offs": striped(np.random.permutation(T)[:S]),
    }


def reference(x_words, x_scales, w1, w2, gamma, offs):
    xq = unpack_fp4(x_words, x_scales)[:, unstriped(offs)]
    h = mxq(f64(w1), 0, "e4m3").T @ xq
    hn = (h - h.mean(axis=1, keepdims=True)) / np.sqrt(h.var(axis=1, keepdims=True) + 1e-5)
    z = relu(f64(gamma) * hn)
    return mxq(f64(w2), 0, "e4m3").T @ mxq(z, 0, "e4m3")

@@ -1,0 +1,171 @@
+from contextlib import ExitStack
+
+import concourse.mybir as mybir
+
+K, T, S, H, N = 512, 1024, 512, 512, 128
+FLOPS = 2 * K * H * S + 2 * H * N * S
+EPS = 1e-5
+
+F32 = mybir.dt.float32
+BF16 = mybir.dt.bfloat16
+I32 = mybir.dt.int32
+U32 = mybir.dt.uint32
+U16 = mybir.dt.uint16
+U8 = mybir.dt.uint8
+FP8X4 = mybir.dt.float8_e4m3fn_x4
+FP4X4 = mybir.dt.float4_e2m1fn_x4
+ACT = mybir.ActivationFunctionType
+ALU = mybir.AluOpType
+
+P = 128
+PACK = 4
+HALF = S // 2
+
+
+def tile_picked_inorm_relu_p_kernel(tc, x_words, x_scales, w1, w2, gamma, offs, out):
+    nc = tc.nc
+    with ExitStack() as ctx:
+        held = ctx.enter_context(tc.tile_pool(name="held", bufs=1))
+        psum = ctx.enter_context(tc.psum_pool(name="psum", bufs=1))
+
+        offsets = held.tile([P, S // 16], U16, name="offsets")
+        word_table = held.tile([P, T], U16, name="word_table", tag="words_then_w2", align_bytes=64)
+        scale_table = held.tile([P, T], U8, name="scale_table", tag="scales_then_w1", align_bytes=64)
+        w1_raw = [held.tile([P, PACK, H // 2], F32, name="w1_raw%d" % c, align_bytes=64) for c in range(2)]
+        warm_in = held.tile([P, 1], F32, name="warm_in", tag="warm_then_gamma")
+        warm_out = held.tile([P, 1], F32, name="warm_out")
+
+        nc.vector.memset(scale_table[:].bitcast(I32), 0)
+        nc.vector.memset(warm_in[:], 1.0)
+        moments = held.tile([P, PACK, 4], F32, name="moments")
+        nc.vector.memset(moments[:], -1.0)
+        nc.sync.dma_start(offsets[:], offs)
+        nc.sync.dma_start(out=word_table[:].bitcast(I32), in_=x_words[0].bitcast(I32))
+        for q in range(4):
+            nc.scalar.dma_start(
+                out=scale_table[32 * q : 32 * q + 4, :].bitcast(I32),
+                in_=x_scales[0][4 * q : 4 * q + 4, :].bitcast(I32),
+            )
+        nc.scalar.activation(warm_out[:], warm_in[:], ACT.Abs_reciprocal_sqrt)
+        w1_rows = w1.rearrange("(p j) c -> p j c", j=PACK)
+        for c in range(2):
+            nc.sync.dma_start(out=w1_raw[c][:], in_=w1_rows[:, :, c * (H // 2) : (c + 1) * (H // 2)])
+        gam = held.tile([P, PACK], F32, name="gam", tag="warm_then_gamma")
+        nc.sync.dma_start(out=gam[:], in_=gamma.rearrange("(p t) o -> p (t o)", t=PACK))
+
+        x_codes = held.tile([P, S], U16, name="x_codes", align_bytes=64)
+        x_sc = held.tile([P, S], U8, name="x_sc", align_bytes=64)
+        nc.vector.tensor_copy(x_codes[:], word_table[:].indirect(offsets[:]))
+        nc.vector.tensor_copy(x_sc[:], scale_table[:].indirect(offsets[:]))
+
+        w2_raw = held.tile([P, PACK, N], F32, name="w2_raw", tag="words_then_w2", align_bytes=64)
+        nc.sync.dma_start(out=w2_raw[:], in_=w2.rearrange("(p j) n -> p j n", j=PACK))
+
+        w1_bf = {}
+
+        def cast_w1(engine_copy, c, u, tag):
+            w1_bf[c, u] = held.tile([P, 2, 64, PACK], BF16, name="w1_bf%d%d" % (c, u), tag=tag, align_bytes=64)
+            src = w1_raw[c][:].rearrange("p j (m t) -> p m j t", t=PACK)[:, :, :, 2 * u : 2 * u + 2]
+            engine_copy(w1_bf[c, u][:].rearrange("p t m j -> p m j t"), src)
+
+        cast_w1(nc.scalar.copy, 0, 0, "w1_bf00")
+        cast_w1(nc.scalar.copy, 0, 1, "w1_bf01")
+        cast_w1(nc.vector.tensor_copy, 1, 0, "scales_then_w1")
+        cast_w1(nc.scalar.copy, 1, 1, "w1_bf11")
+
+        h = []
+        for t in range(PACK):
+            codes = held.tile([P, P], U32, name="w1_codes%d" % t, align_bytes=64)
+            scales = held.tile([P, P], U8, name="w1_scales%d" % t, align_bytes=64)
+            for c in range(2):
+                nc.vector.quantize_mx(
+                    out=codes[:, c * 64 : (c + 1) * 64].bitcast(FP8X4),
+                    scales=scales[:, c * 64 : (c + 1) * 64],
+                    in_=w1_bf[c, t // 2][:, t % 2].rearrange("p m j -> p (m j)"),
+                )
+            bank = psum.tile([P, S], F32, name="h%d" % t)
+            nc.tensor.matmul_mx(
+                out=bank[:],
+                lhsT=codes[:].bitcast(FP8X4),
+                lhsT_scale=scales[:],
+                rhs=x_codes[:].bitcast(FP4X4),
+                rhs_scale=x_sc[:],
+                start=True,
+                stop=True,
+            )
+            h.append(bank)
+
+        w2_bf = held.tile([P, N, PACK], BF16, name="w2_bf", align_bytes=64)
+        nc.scalar.copy(
+            w2_bf[:].rearrange("p (c i) j -> p c j i", i=4),
+            w2_raw[:].rearrange("p j (c i) -> p c j i", i=4),
+        )
+        w2_codes = held.tile([P, N], U32, name="w2_codes", align_bytes=64)
+        w2_scales = held.tile([P, N], U8, name="w2_scales", align_bytes=64)
+
+        planes = held.tile([P, PACK, S], BF16, name="planes", align_bytes=64)
+        coef = []
+        for t in range(PACK):
+            stats = held.tile([P, 6], F32, name="stats%d" % t)
+            rstd = held.tile([P, 1], F32, name="rstd%d" % t)
+            nc.vector.bn_stats(stats[:], h[t][:])
+            nc.vector.bn_aggr(moments[:, t, 1:3], stats[:])
+            nc.scalar.activation(rstd[:], moments[:, t, 2:3], ACT.Abs_reciprocal_sqrt, bias=EPS)
+            if t in (0, 3):
+                gc = held.tile([P, 2], F32, name="gc%d" % t)
+                ab = held.tile([P, 2], F32, name="ab%d" % t)
+                nc.vector.tensor_scalar(gc[:], moments[:, t, 0:2], gam[:, t : t + 1], -1.0, ALU.mult, ALU.mult)
+                nc.scalar.activation(ab[:], gc[:], ACT.Copy, scale=rstd[:])
+            else:
+                ab = held.tile([P, 1], F32, name="ab%d" % t)
+                nc.scalar.activation(ab[:], gam[:, t : t + 1], ACT.Copy, scale=rstd[:])
+            coef.append(ab)
+        for t in range(PACK):
+            ab = coef[t]
+            if t in (0, 3):
+                for lo in (0, HALF):
+                    nc.scalar.activation(
+                        planes[:, t, lo : lo + HALF], h[t][:, lo : lo + HALF], ACT.Identity, bias=ab[:, 1:2], scale=ab[:, 0:1]
+                    )
+            else:
+                nc.vector.tensor_scalar(
+                    planes[:, t, :], h[t][:], moments[:, t, 1:2], ab[:], ALU.subtract, ALU.mult
+                )
+
+        nc.vector.quantize_mx(
+            out=w2_codes[:].bitcast(FP8X4), scales=w2_scales[:], in_=w2_bf[:].rearrange("p n j -> p (n j)")
+        )
+
+        chunks = [(0, 256), (256, 384), (384, 512)]
+        z_bf = [held.tile([P, hi - lo, PACK], BF16, name="z_bf%d" % lo, align_bytes=64) for lo, hi in chunks]
+        for s, (lo, hi) in enumerate(chunks):
+            dst = z_bf[s][:].rearrange("p (c i) t -> p c t i", i=4)
+            src = planes[:, :, lo:hi].rearrange("p t (c i) -> p c t i", i=4)
+            if s == 1:
+                nc.scalar.activation(dst, src, ACT.Relu)
+            else:
+                nc.vector.tensor_scalar_max(dst, src, 0.0)
+
+        for s in (0, 2, 1):
+            lo, hi = chunks[s]
+            z_codes = held.tile([P, hi - lo], U32, name="z_codes%d" % s, align_bytes=64)
+            z_scales = held.tile([P, hi - lo], U8, name="z_scales%d" % s, align_bytes=64)
+            nc.vector.quantize_mx(
+                out=z_codes[:].bitcast(FP8X4), scales=z_scales[:], in_=z_bf[s][:].rearrange("p n t -> p (n t)")
+            )
+            acc = psum.tile([P, hi - lo], F32, name="acc%d" % s)
+            nc.tensor.matmul_mx(
+                out=acc[:],
+                lhsT=w2_codes[:].bitcast(FP8X4),
+                lhsT_scale=w2_scales[:],
+                rhs=z_codes[:].bitcast(FP8X4),
+                rhs_scale=z_scales[:],
+                start=True,
+                stop=True,
+            )
+            result = held.tile([P, hi - lo], F32, name="result%d" % s)
+            if s == 1:
+                nc.vector.tensor_copy(result[:], acc[:])
+            else:
+                nc.scalar.copy(result[:], acc[:])
+            nc.sync.dma_start(out=out[:, lo:hi], in_=result[:])

@@ -37,12 +37,11 @@ def tile_picked_inorm_relu_p_kernel(tc, x_words, x_scales, w1, w2, gamma, offs, 
 
         nc.vector.memset(scale_table[:].bitcast(I32), 0)
         nc.vector.memset(warm_in[:], 1.0)
-        moments = held.tile([P, PACK, 4], F32, name="moments")
-        nc.vector.memset(moments[:], -1.0)
+        moments = held.tile([P, PACK, 2], F32, name="moments")
         nc.sync.dma_start(offsets[:], offs)
-        nc.sync.dma_start(out=word_table[:].bitcast(I32), in_=x_words[0].bitcast(I32))
+        nc.scalar.dma_start(out=word_table[:].bitcast(I32), in_=x_words[0].bitcast(I32))
         for q in range(4):
-            nc.scalar.dma_start(
+            (nc.sync if q < 2 else nc.scalar).dma_start(
                 out=scale_table[32 * q : 32 * q + 4, :].bitcast(I32),
                 in_=x_scales[0][4 * q : 4 * q + 4, :].bitcast(I32),
             )
@@ -61,27 +60,32 @@ def tile_picked_inorm_relu_p_kernel(tc, x_words, x_scales, w1, w2, gamma, offs, 
         w2_raw = held.tile([P, PACK, N], F32, name="w2_raw", tag="words_then_w2", align_bytes=64)
         nc.sync.dma_start(out=w2_raw[:], in_=w2.rearrange("(p j) n -> p j n", j=PACK))
 
-        w1_bf = {}
+        early01 = held.tile([P, 2, 64, PACK], BF16, name="early01", align_bytes=64)
+        late01 = held.tile([P, 2, 64, PACK], BF16, name="late01", tag="scales_then_w1", align_bytes=64)
+        whole23 = held.tile([P, 2, P, PACK], BF16, name="whole23", align_bytes=64)
 
-        def cast_w1(engine_copy, c, u, tag):
-            w1_bf[c, u] = held.tile([P, 2, 64, PACK], BF16, name="w1_bf%d%d" % (c, u), tag=tag, align_bytes=64)
+        def cast_w1(engine_copy, dst, c, u):
             src = w1_raw[c][:].rearrange("p j (m t) -> p m j t", t=PACK)[:, :, :, 2 * u : 2 * u + 2]
-            engine_copy(w1_bf[c, u][:].rearrange("p t m j -> p m j t"), src)
+            engine_copy(dst.rearrange("p t m j -> p m j t"), src)
 
-        cast_w1(nc.scalar.copy, 0, 0, "w1_bf00")
-        cast_w1(nc.scalar.copy, 0, 1, "w1_bf01")
-        cast_w1(nc.vector.tensor_copy, 1, 0, "scales_then_w1")
-        cast_w1(nc.scalar.copy, 1, 1, "w1_bf11")
+        cast_w1(nc.scalar.copy, early01[:], 0, 0)
+        cast_w1(nc.scalar.copy, whole23[:, :, 0:64, :], 0, 1)
+        cast_w1(nc.vector.tensor_copy, late01[:], 1, 0)
+        cast_w1(nc.scalar.copy, whole23[:, :, 64:128, :], 1, 1)
 
         h = []
         for t in range(PACK):
             codes = held.tile([P, P], U32, name="w1_codes%d" % t, align_bytes=64)
             scales = held.tile([P, P], U8, name="w1_scales%d" % t, align_bytes=64)
-            for c in range(2):
+            if t < 2:
+                pieces = [(slice(0, 64), early01[:, t]), (slice(64, 128), late01[:, t])]
+            else:
+                pieces = [(slice(0, 128), whole23[:, t - 2])]
+            for cols, values in pieces:
                 nc.vector.quantize_mx(
-                    out=codes[:, c * 64 : (c + 1) * 64].bitcast(FP8X4),
-                    scales=scales[:, c * 64 : (c + 1) * 64],
-                    in_=w1_bf[c, t // 2][:, t % 2].rearrange("p m j -> p (m j)"),
+                    out=codes[:, cols].bitcast(FP8X4),
+                    scales=scales[:, cols],
+                    in_=values.rearrange("p m j -> p (m j)"),
                 )
             bank = psum.tile([P, S], F32, name="h%d" % t)
             nc.tensor.matmul_mx(
@@ -95,6 +99,10 @@ def tile_picked_inorm_relu_p_kernel(tc, x_words, x_scales, w1, w2, gamma, offs, 
             )
             h.append(bank)
 
+        half_neg_gam = held.tile([P, PACK], F32, name="half_neg_gam")
+        nc.scalar.activation(half_neg_gam[:], gam[:], ACT.Copy, scale=-0.5)
+        gc = held.tile([P, PACK, 2], F32, name="gc")
+        nc.scalar.copy(gc[:, :, 0], gam[:])
         w2_bf = held.tile([P, N, PACK], BF16, name="w2_bf", align_bytes=64)
         nc.scalar.copy(
             w2_bf[:].rearrange("p (c i) j -> p c j i", i=4),
@@ -103,33 +111,33 @@ def tile_picked_inorm_relu_p_kernel(tc, x_words, x_scales, w1, w2, gamma, offs, 
         w2_codes = held.tile([P, N], U32, name="w2_codes", align_bytes=64)
         w2_scales = held.tile([P, N], U8, name="w2_scales", align_bytes=64)
 
-        planes = held.tile([P, PACK, S], BF16, name="planes", align_bytes=64)
+        planes = [held.tile([P, PACK, HALF], BF16, name="planes%d" % s, align_bytes=64) for s in range(2)]
         coef = []
         for t in range(PACK):
             stats = held.tile([P, 6], F32, name="stats%d" % t)
             rstd = held.tile([P, 1], F32, name="rstd%d" % t)
             nc.vector.bn_stats(stats[:], h[t][:])
-            nc.vector.bn_aggr(moments[:, t, 1:3], stats[:])
-            nc.scalar.activation(rstd[:], moments[:, t, 2:3], ACT.Abs_reciprocal_sqrt, bias=EPS)
-            if t in (0, 3):
-                gc = held.tile([P, 2], F32, name="gc%d" % t)
+            nc.vector.bn_aggr(moments[:, t, :], stats[:])
+            nc.scalar.activation(rstd[:], moments[:, t, 1:2], ACT.Abs_reciprocal_sqrt, bias=EPS)
+            if t != 1:
                 ab = held.tile([P, 2], F32, name="ab%d" % t)
-                nc.vector.tensor_scalar(gc[:], moments[:, t, 0:2], gam[:, t : t + 1], -1.0, ALU.mult, ALU.mult)
-                nc.scalar.activation(ab[:], gc[:], ACT.Copy, scale=rstd[:])
+                nc.vector.tensor_scalar(
+                    gc[:, t, 1:2], stats[:, 1:2], stats[:, 4:5], half_neg_gam[:, t : t + 1], ALU.add, ALU.mult
+                )
+                nc.scalar.activation(ab[:], gc[:, t, :], ACT.Copy, scale=rstd[:])
             else:
                 ab = held.tile([P, 1], F32, name="ab%d" % t)
                 nc.scalar.activation(ab[:], gam[:, t : t + 1], ACT.Copy, scale=rstd[:])
             coef.append(ab)
-        for t in range(PACK):
+        for t, s, on_scalar in [(0, 0, True), (0, 1, True), (1, 0, False), (1, 1, False), (2, 0, False),
+                                (3, 0, True), (2, 1, True), (3, 1, True)]:
             ab = coef[t]
-            if t in (0, 3):
-                for lo in (0, HALF):
-                    nc.scalar.activation(
-                        planes[:, t, lo : lo + HALF], h[t][:, lo : lo + HALF], ACT.Identity, bias=ab[:, 1:2], scale=ab[:, 0:1]
-                    )
+            src = h[t][:, s * HALF : (s + 1) * HALF]
+            if on_scalar:
+                nc.scalar.activation(planes[s][:, t, :], src, ACT.Identity, bias=ab[:, 1:2], scale=ab[:, 0:1])
             else:
                 nc.vector.tensor_scalar(
-                    planes[:, t, :], h[t][:], moments[:, t, 1:2], ab[:], ALU.subtract, ALU.mult
+                    planes[s][:, t, :], src, moments[:, t, 0:1], ab[:, 0:1], ALU.subtract, ALU.mult
                 )
 
         nc.vector.quantize_mx(
@@ -140,7 +148,7 @@ def tile_picked_inorm_relu_p_kernel(tc, x_words, x_scales, w1, w2, gamma, offs, 
         z_bf = [held.tile([P, hi - lo, PACK], BF16, name="z_bf%d" % lo, align_bytes=64) for lo, hi in chunks]
         for s, (lo, hi) in enumerate(chunks):
             dst = z_bf[s][:].rearrange("p (c i) t -> p c t i", i=4)
-            src = planes[:, :, lo:hi].rearrange("p t (c i) -> p c t i", i=4)
+            src = planes[lo // HALF][:, :, lo % HALF : lo % HALF + hi - lo].rearrange("p t (c i) -> p c t i", i=4)
             if s == 1:
                 nc.scalar.activation(dst, src, ACT.Relu)
             else:

@@ -144,24 +144,25 @@ def tile_picked_inorm_relu_p_kernel(tc, x_words, x_scales, w1, w2, gamma, offs, 
             out=w2_codes[:].bitcast(FP8X4), scales=w2_scales[:], in_=w2_bf[:].rearrange("p n j -> p (n j)")
         )
 
-        chunks = [(0, 256), (256, 384), (384, 512)]
-        z_bf = [held.tile([P, hi - lo, PACK], BF16, name="z_bf%d" % lo, align_bytes=64) for lo, hi in chunks]
-        for s, (lo, hi) in enumerate(chunks):
-            dst = z_bf[s][:].rearrange("p (c i) t -> p c t i", i=4)
-            src = planes[lo // HALF][:, :, lo % HALF : lo % HALF + hi - lo].rearrange("p t (c i) -> p c t i", i=4)
-            if s == 1:
+        quarter = S // 4
+        z_bf = [held.tile([P, quarter, PACK], BF16, name="z_bf%d" % c, align_bytes=64) for c in range(4)]
+
+        def weave(c):
+            lo = (c % 2) * quarter
+            dst = z_bf[c][:].rearrange("p (g i) t -> p g t i", i=4)
+            src = planes[c // 2][:, :, lo : lo + quarter].rearrange("p t (g i) -> p g t i", i=4)
+            if c == 2:
                 nc.scalar.activation(dst, src, ACT.Relu)
             else:
                 nc.vector.tensor_scalar_max(dst, src, 0.0)
 
-        for s in (0, 2, 1):
-            lo, hi = chunks[s]
-            z_codes = held.tile([P, hi - lo], U32, name="z_codes%d" % s, align_bytes=64)
-            z_scales = held.tile([P, hi - lo], U8, name="z_scales%d" % s, align_bytes=64)
+        def second_layer(c, engine_copy):
+            z_codes = held.tile([P, quarter], U32, name="z_codes%d" % c, align_bytes=64)
+            z_scales = held.tile([P, quarter], U8, name="z_scales%d" % c, align_bytes=64)
             nc.vector.quantize_mx(
-                out=z_codes[:].bitcast(FP8X4), scales=z_scales[:], in_=z_bf[s][:].rearrange("p n t -> p (n t)")
+                out=z_codes[:].bitcast(FP8X4), scales=z_scales[:], in_=z_bf[c][:].rearrange("p n t -> p (n t)")
             )
-            acc = psum.tile([P, hi - lo], F32, name="acc%d" % s)
+            acc = psum.tile([P, quarter], F32, name="acc%d" % c)
             nc.tensor.matmul_mx(
                 out=acc[:],
                 lhsT=w2_codes[:].bitcast(FP8X4),
@@ -171,9 +172,15 @@ def tile_picked_inorm_relu_p_kernel(tc, x_words, x_scales, w1, w2, gamma, offs, 
                 start=True,
                 stop=True,
             )
-            result = held.tile([P, hi - lo], F32, name="result%d" % s)
-            if s == 1:
-                nc.vector.tensor_copy(result[:], acc[:])
-            else:
-                nc.scalar.copy(result[:], acc[:])
-            nc.sync.dma_start(out=out[:, lo:hi], in_=result[:])
+            result = held.tile([P, quarter], F32, name="result%d" % c)
+            engine_copy(result[:], acc[:])
+            nc.sync.dma_start(out=out[:, c * quarter : (c + 1) * quarter], in_=result[:])
+
+        weave(0)
+        weave(1)
+        weave(2)
+        second_layer(0, nc.scalar.copy)
+        weave(3)
+        second_layer(1, nc.vector.tensor_copy)
+        second_layer(3, nc.scalar.copy)
+        second_layer(2, nc.vector.tensor_copy)

@@ -30,8 +30,8 @@ def tile_picked_inorm_relu_p_kernel(tc, x_words, x_scales, w1, w2, gamma, offs, 
 
         offsets = held.tile([P, S // 16], U16, name="offsets")
         word_table = held.tile([P, T], U16, name="word_table", tag="words_then_w2", align_bytes=64)
-        scale_table = held.tile([P, T], U8, name="scale_table", tag="scales_then_w1", align_bytes=64)
-        w1_raw = [held.tile([P, PACK, H // 2], F32, name="w1_raw%d" % c, align_bytes=64) for c in range(2)]
+        scale_table = held.tile([P, T], U8, name="scale_table", align_bytes=64)
+        w1_raw = [held.tile([P, 2, H], F32, name="w1_raw%d" % c, align_bytes=64) for c in range(2)]
         warm_in = held.tile([P, 1], F32, name="warm_in", tag="warm_then_gamma")
         warm_out = held.tile([P, 1], F32, name="warm_out")
 
@@ -48,7 +48,7 @@ def tile_picked_inorm_relu_p_kernel(tc, x_words, x_scales, w1, w2, gamma, offs, 
         nc.scalar.activation(warm_out[:], warm_in[:], ACT.Abs_reciprocal_sqrt)
         w1_rows = w1.rearrange("(p j) c -> p j c", j=PACK)
         for c in range(2):
-            nc.sync.dma_start(out=w1_raw[c][:], in_=w1_rows[:, :, c * (H // 2) : (c + 1) * (H // 2)])
+            nc.sync.dma_start(out=w1_raw[c][:], in_=w1_rows[:, 2 * c : 2 * c + 2, :])
         gam = held.tile([P, PACK], F32, name="gam", tag="warm_then_gamma")
         nc.sync.dma_start(out=gam[:], in_=gamma.rearrange("(p t) o -> p (t o)", t=PACK))
 
@@ -60,33 +60,26 @@ def tile_picked_inorm_relu_p_kernel(tc, x_words, x_scales, w1, w2, gamma, offs, 
         w2_raw = held.tile([P, PACK, N], F32, name="w2_raw", tag="words_then_w2", align_bytes=64)
         nc.sync.dma_start(out=w2_raw[:], in_=w2.rearrange("(p j) n -> p j n", j=PACK))
 
-        early01 = held.tile([P, 2, 64, PACK], BF16, name="early01", align_bytes=64)
-        late01 = held.tile([P, 2, 64, PACK], BF16, name="late01", tag="scales_then_w1", align_bytes=64)
-        whole23 = held.tile([P, 2, P, PACK], BF16, name="whole23", align_bytes=64)
+        w1_bf = [held.tile([P, 2, P, PACK], BF16, name="w1_bf%d" % u, align_bytes=64) for u in range(2)]
 
-        def cast_w1(engine_copy, dst, c, u):
+        def cast_w1(engine_copy, c, u):
             src = w1_raw[c][:].rearrange("p j (m t) -> p m j t", t=PACK)[:, :, :, 2 * u : 2 * u + 2]
-            engine_copy(dst.rearrange("p t m j -> p m j t"), src)
+            engine_copy(w1_bf[u][:, :, :, 2 * c : 2 * c + 2].rearrange("p t m j -> p m j t"), src)
 
-        cast_w1(nc.scalar.copy, early01[:], 0, 0)
-        cast_w1(nc.scalar.copy, whole23[:, :, 0:64, :], 0, 1)
-        cast_w1(nc.vector.tensor_copy, late01[:], 1, 0)
-        cast_w1(nc.scalar.copy, whole23[:, :, 64:128, :], 1, 1)
+        cast_w1(nc.scalar.copy, 0, 0)
+        cast_w1(nc.scalar.copy, 0, 1)
+        cast_w1(nc.vector.tensor_copy, 1, 0)
+        cast_w1(nc.scalar.copy, 1, 1)
 
         h = []
         for t in range(PACK):
             codes = held.tile([P, P], U32, name="w1_codes%d" % t, align_bytes=64)
             scales = held.tile([P, P], U8, name="w1_scales%d" % t, align_bytes=64)
-            if t < 2:
-                pieces = [(slice(0, 64), early01[:, t]), (slice(64, 128), late01[:, t])]
-            else:
-                pieces = [(slice(0, 128), whole23[:, t - 2])]
-            for cols, values in pieces:
-                nc.vector.quantize_mx(
-                    out=codes[:, cols].bitcast(FP8X4),
-                    scales=scales[:, cols],
-                    in_=values.rearrange("p m j -> p (m j)"),
-                )
+            nc.vector.quantize_mx(
+                out=codes[:].bitcast(FP8X4),
+                scales=scales[:],
+                in_=w1_bf[t // 2][:, t % 2].rearrange("p m j -> p (m j)"),
+            )
             bank = psum.tile([P, S], F32, name="h%d" % t)
             nc.tensor.matmul_mx(
                 out=bank[:],
@@ -174,7 +167,7 @@ def tile_picked_inorm_relu_p_kernel(tc, x_words, x_scales, w1, w2, gamma, offs, 
             )
             result = held.tile([P, quarter], F32, name="result%d" % c)
             engine_copy(result[:], acc[:])
-            nc.sync.dma_start(out=out[:, c * quarter : (c + 1) * quarter], in_=result[:])
+            (nc.scalar if c == 3 else nc.sync).dma_start(out=out[:, c * quarter : (c + 1) * quarter], in_=result[:])
 
         weave(0)
         weave(1)

@@ -31,7 +31,7 @@ def tile_picked_inorm_relu_p_kernel(tc, x_words, x_scales, w1, w2, gamma, offs, 
         offsets = held.tile([P, S // 16], U16, name="offsets")
         word_table = held.tile([P, T], U16, name="word_table", tag="words_then_w2", align_bytes=64)
         scale_table = held.tile([P, T], U8, name="scale_table", align_bytes=64)
-        w1_raw = [held.tile([P, 2, H], F32, name="w1_raw%d" % c, align_bytes=64) for c in range(2)]
+        w1_raw = [held.tile([P, 2, H], F32, name="w1_raw%d" % c, tag="w1_raw%d" % c, align_bytes=64) for c in range(2)]
         warm_in = held.tile([P, 1], F32, name="warm_in", tag="warm_then_gamma")
         warm_out = held.tile([P, 1], F32, name="warm_out")
 
@@ -62,14 +62,16 @@ def tile_picked_inorm_relu_p_kernel(tc, x_words, x_scales, w1, w2, gamma, offs, 
 
         w1_bf = [held.tile([P, 2, P, PACK], BF16, name="w1_bf%d" % u, align_bytes=64) for u in range(2)]
 
-        def cast_w1(engine_copy, c, u):
-            src = w1_raw[c][:].rearrange("p j (m t) -> p m j t", t=PACK)[:, :, :, 2 * u : 2 * u + 2]
-            engine_copy(w1_bf[u][:, :, :, 2 * c : 2 * c + 2].rearrange("p t m j -> p m j t"), src)
+        def cast_w1(engine_copy, c, lo, hi):
+            src = w1_raw[c][:].rearrange("p j (m t) -> p m j t", t=PACK)[:, :, :, lo:hi]
+            dst = w1_bf[lo // 2][:, lo % 2 : lo % 2 + hi - lo, :, 2 * c : 2 * c + 2]
+            engine_copy(dst.rearrange("p t m j -> p m j t"), src)
 
-        cast_w1(nc.scalar.copy, 0, 0)
-        cast_w1(nc.scalar.copy, 0, 1)
-        cast_w1(nc.vector.tensor_copy, 1, 0)
-        cast_w1(nc.scalar.copy, 1, 1)
+        cast_w1(nc.scalar.copy, 0, 0, 2)
+        cast_w1(nc.scalar.copy, 0, 2, 4)
+        cast_w1(nc.vector.tensor_copy, 1, 0, 2)
+        cast_w1(nc.vector.tensor_copy, 1, 2, 3)
+        cast_w1(nc.scalar.copy, 1, 3, 4)
 
         h = []
         for t in range(PACK):
@@ -80,82 +82,101 @@ def tile_picked_inorm_relu_p_kernel(tc, x_words, x_scales, w1, w2, gamma, offs, 
                 scales=scales[:],
                 in_=w1_bf[t // 2][:, t % 2].rearrange("p m j -> p (m j)"),
             )
-            bank = psum.tile([P, S], F32, name="h%d" % t)
-            nc.tensor.matmul_mx(
-                out=bank[:],
-                lhsT=codes[:].bitcast(FP8X4),
-                lhsT_scale=scales[:],
-                rhs=x_codes[:].bitcast(FP4X4),
-                rhs_scale=x_sc[:],
-                start=True,
-                stop=True,
-            )
-            h.append(bank)
+            banks = []
+            for s in range(2):
+                bank = psum.tile([P, HALF], F32, name="h%d_%d" % (t, s), tag="bank%d" % (2 * t + s))
+                nc.tensor.matmul_mx(
+                    out=bank[:],
+                    lhsT=codes[:].bitcast(FP8X4),
+                    lhsT_scale=scales[:],
+                    rhs=x_codes[:, s * HALF : (s + 1) * HALF].bitcast(FP4X4),
+                    rhs_scale=x_sc[:, s * HALF : (s + 1) * HALF],
+                    start=True,
+                    stop=True,
+                )
+                banks.append(bank)
+            h.append(banks)
 
-        half_neg_gam = held.tile([P, PACK], F32, name="half_neg_gam")
-        nc.scalar.activation(half_neg_gam[:], gam[:], ACT.Copy, scale=-0.5)
+        neg_gam = held.tile([P, PACK], F32, name="neg_gam")
+        nc.scalar.activation(neg_gam[:], gam[:], ACT.Copy, scale=-1.0)
         gc = held.tile([P, PACK, 2], F32, name="gc")
         nc.scalar.copy(gc[:, :, 0], gam[:])
-        w2_bf = held.tile([P, N, PACK], BF16, name="w2_bf", align_bytes=64)
+        w2_bf = held.tile([P, N, PACK], BF16, name="w2_bf", tag="w1_raw1", align_bytes=64)
         nc.scalar.copy(
             w2_bf[:].rearrange("p (c i) j -> p c j i", i=4),
             w2_raw[:].rearrange("p j (c i) -> p c j i", i=4),
         )
-        w2_codes = held.tile([P, N], U32, name="w2_codes", align_bytes=64)
         w2_scales = held.tile([P, N], U8, name="w2_scales", align_bytes=64)
 
         planes = [held.tile([P, PACK, HALF], BF16, name="planes%d" % s, align_bytes=64) for s in range(2)]
         coef = []
+        early = held.tile([P, 3, 6], F32, name="stats01")
+        third = held.tile([P, 2, 6], F32, name="stats2", tag="stats_then_w2", align_bytes=64)
+        last = held.tile([P, 2, 6], F32, name="stats3")
+        rows = [(0, 1), (2, 1), (0, 1), (0, 1)]
         for t in range(PACK):
-            stats = held.tile([P, 6], F32, name="stats%d" % t)
+            stats = [early, early, third, last][t]
             rstd = held.tile([P, 1], F32, name="rstd%d" % t)
-            nc.vector.bn_stats(stats[:], h[t][:])
-            nc.vector.bn_aggr(moments[:, t, :], stats[:])
+            for s in range(2):
+                nc.vector.bn_stats(stats[:, rows[t][s], :], h[t][s][:])
+            first = min(rows[t])
+            nc.vector.bn_aggr(moments[:, t, :], stats[:, first : first + 2, :].rearrange("p s v -> p (s v)"))
             nc.scalar.activation(rstd[:], moments[:, t, 1:2], ACT.Abs_reciprocal_sqrt, bias=EPS)
-            if t != 1:
+            if t != 2:
                 ab = held.tile([P, 2], F32, name="ab%d" % t)
-                nc.vector.tensor_scalar(
-                    gc[:, t, 1:2], stats[:, 1:2], stats[:, 4:5], half_neg_gam[:, t : t + 1], ALU.add, ALU.mult
-                )
+                nc.scalar.activation(gc[:, t, 1:2], moments[:, t, 0:1], ACT.Copy, scale=neg_gam[:, t : t + 1])
                 nc.scalar.activation(ab[:], gc[:, t, :], ACT.Copy, scale=rstd[:])
             else:
                 ab = held.tile([P, 1], F32, name="ab%d" % t)
                 nc.scalar.activation(ab[:], gam[:, t : t + 1], ACT.Copy, scale=rstd[:])
             coef.append(ab)
-        for t, s, on_scalar in [(0, 0, True), (0, 1, True), (1, 0, False), (1, 1, False), (2, 0, False),
-                                (3, 0, True), (2, 1, True), (3, 1, True)]:
-            ab = coef[t]
-            src = h[t][:, s * HALF : (s + 1) * HALF]
-            if on_scalar:
-                nc.scalar.activation(planes[s][:, t, :], src, ACT.Identity, bias=ab[:, 1:2], scale=ab[:, 0:1])
-            else:
-                nc.vector.tensor_scalar(
-                    planes[s][:, t, :], src, moments[:, t, 0:1], ab[:, 0:1], ALU.subtract, ALU.mult
-                )
 
+        def norm_scalar(t, s, lo=0, hi=HALF):
+            ab = coef[t]
+            nc.scalar.activation(
+                planes[s][:, t, lo:hi], h[t][s][:, lo:hi], ACT.Identity, bias=ab[:, 1:2], scale=ab[:, 0:1]
+            )
+
+        def norm_vector(t, s, lo, hi):
+            nc.vector.tensor_scalar(
+                planes[s][:, t, lo:hi], h[t][s][:, lo:hi], moments[:, t, 0:1], coef[t][:, 0:1], ALU.subtract, ALU.mult
+            )
+
+        for t in range(2):
+            for s in range(2):
+                norm_scalar(t, s)
+        norm_vector(2, 0, 0, HALF)
+        norm_vector(2, 1, 0, HALF)
+        norm_scalar(3, 1, 0, HALF // 2)
+        norm_scalar(3, 1, HALF // 2, HALF)
+        norm_vector(3, 0, 0, HALF // 2)
+        norm_vector(3, 0, HALF // 2, HALF)
+
+        w2_codes = held.tile([P, N], U32, name="w2_codes", tag="stats_then_w2", align_bytes=64)
         nc.vector.quantize_mx(
             out=w2_codes[:].bitcast(FP8X4), scales=w2_scales[:], in_=w2_bf[:].rearrange("p n j -> p (n j)")
         )
 
-        quarter = S // 4
-        z_bf = [held.tile([P, quarter, PACK], BF16, name="z_bf%d" % c, align_bytes=64) for c in range(4)]
+        chunks = [(0, 128), (128, 256), (256, 384), (384, 512)]
+        z_bf = [held.tile([P, hi - lo, PACK], BF16, name="z_bf%d" % lo, align_bytes=64) for lo, hi in chunks]
 
-        def weave(c):
-            lo = (c % 2) * quarter
-            dst = z_bf[c][:].rearrange("p (g i) t -> p g t i", i=4)
-            src = planes[c // 2][:, :, lo : lo + quarter].rearrange("p t (g i) -> p g t i", i=4)
-            if c == 2:
+        def weave(c, lo, hi, on_scalar):
+            base = chunks[c][0]
+            dst = z_bf[c][:, lo - base : hi - base, :].rearrange("p (g i) t -> p g t i", i=4)
+            src = planes[lo // HALF][:, :, lo % HALF : lo % HALF + hi - lo].rearrange("p t (g i) -> p g t i", i=4)
+            if on_scalar:
                 nc.scalar.activation(dst, src, ACT.Relu)
             else:
                 nc.vector.tensor_scalar_max(dst, src, 0.0)
 
-        def second_layer(c, engine_copy):
-            z_codes = held.tile([P, quarter], U32, name="z_codes%d" % c, align_bytes=64)
-            z_scales = held.tile([P, quarter], U8, name="z_scales%d" % c, align_bytes=64)
+        def second_layer(c, engine_copy, queue):
+            lo, hi = chunks[c]
+            z_codes = held.tile([P, hi - lo], U32, name="z_codes%d" % c, align_bytes=64)
+            z_scales = held.tile([P, hi - lo], U8, name="z_scales%d" % c, align_bytes=64)
             nc.vector.quantize_mx(
                 out=z_codes[:].bitcast(FP8X4), scales=z_scales[:], in_=z_bf[c][:].rearrange("p n t -> p (n t)")
             )
-            acc = psum.tile([P, quarter], F32, name="acc%d" % c)
+            acc = psum.tile([P, hi - lo], F32, name="acc%d" % c, tag="bank%d" % c)
             nc.tensor.matmul_mx(
                 out=acc[:],
                 lhsT=w2_codes[:].bitcast(FP8X4),
@@ -165,15 +186,15 @@ def tile_picked_inorm_relu_p_kernel(tc, x_words, x_scales, w1, w2, gamma, offs, 
                 start=True,
                 stop=True,
             )
-            result = held.tile([P, quarter], F32, name="result%d" % c)
+            result = held.tile([P, hi - lo], F32, name="result%d" % c)
             engine_copy(result[:], acc[:])
-            (nc.scalar if c == 3 else nc.sync).dma_start(out=out[:, c * quarter : (c + 1) * quarter], in_=result[:])
+            queue.dma_start(out=out[:, lo:hi], in_=result[:])
 
-        weave(0)
-        weave(1)
-        weave(2)
-        second_layer(0, nc.scalar.copy)
-        weave(3)
-        second_layer(1, nc.vector.tensor_copy)
-        second_layer(3, nc.scalar.copy)
-        second_layer(2, nc.vector.tensor_copy)
+        weave(0, 0, 128, False)
+        weave(1, 128, 256, False)
+        weave(2, 256, 384, True)
+        weave(3, 384, 512, True)
+        second_layer(0, nc.scalar.copy, nc.sync)
+        second_layer(1, nc.scalar.copy, nc.sync)
+        second_layer(2, nc.scalar.copy, nc.scalar)
+        second_layer(3, nc.vector.tensor_copy, nc.sync)

@@ -35,7 +35,7 @@ def tile_picked_inorm_relu_p_kernel(tc, x_words, x_scales, w1, w2, gamma, offs, 
         warm_in = held.tile([P, 1], F32, name="warm_in", tag="warm_then_gamma")
         warm_out = held.tile([P, 1], F32, name="warm_out")
 
-        nc.vector.memset(scale_table[:].bitcast(I32), 0)
+        nc.gpsimd.memset(scale_table[:].bitcast(I32), 0)
         nc.vector.memset(warm_in[:], 1.0)
         moments = held.tile([P, PACK, 2], F32, name="moments")
         nc.sync.dma_start(offsets[:], offs)
@@ -110,10 +110,10 @@ def tile_picked_inorm_relu_p_kernel(tc, x_words, x_scales, w1, w2, gamma, offs, 
 
         planes = [held.tile([P, PACK, HALF], BF16, name="planes%d" % s, align_bytes=64) for s in range(2)]
         coef = []
-        early = held.tile([P, 3, 6], F32, name="stats01")
+        early = held.tile([P, 4, 6], F32, name="stats01")
         third = held.tile([P, 2, 6], F32, name="stats2", tag="stats_then_w2", align_bytes=64)
         last = held.tile([P, 2, 6], F32, name="stats3")
-        rows = [(0, 1), (2, 1), (0, 1), (0, 1)]
+        rows = [(0, 1), (2, 3), (0, 1), (0, 1)]
         for t in range(PACK):
             stats = [early, early, third, last][t]
             rstd = held.tile([P, 1], F32, name="rstd%d" % t)

@@ -193,8 +193,9 @@ def tile_picked_inorm_relu_p_kernel(tc, x_words, x_scales, w1, w2, gamma, offs, 
         weave(0, 0, 128, False)
         weave(1, 128, 256, False)
         weave(2, 256, 384, True)
-        weave(3, 384, 512, True)
+        weave(3, 384, 448, True)
         second_layer(0, nc.scalar.copy, nc.sync)
+        weave(3, 448, 512, False)
         second_layer(1, nc.scalar.copy, nc.sync)
         second_layer(2, nc.scalar.copy, nc.scalar)
         second_layer(3, nc.vector.tensor_copy, nc.sync)

@@ -68,10 +68,10 @@ def tile_picked_inorm_relu_p_kernel(tc, x_words, x_scales, w1, w2, gamma, offs, 
             engine_copy(dst.rearrange("p t m j -> p m j t"), src)
 
         cast_w1(nc.scalar.copy, 0, 0, 2)
-        cast_w1(nc.scalar.copy, 0, 2, 4)
-        cast_w1(nc.vector.tensor_copy, 1, 0, 2)
-        cast_w1(nc.vector.tensor_copy, 1, 2, 3)
-        cast_w1(nc.scalar.copy, 1, 3, 4)
+        cast_w1(nc.vector.tensor_copy, 0, 2, 4)
+        cast_w1(nc.vector.tensor_copy, 1, 0, 1)
+        cast_w1(nc.vector.tensor_copy, 1, 1, 2)
+        cast_w1(nc.scalar.copy, 1, 2, 4)
 
         h = []
         for t in range(PACK):

@@ -62,33 +62,36 @@ def tile_picked_inorm_relu_p_kernel(tc, x_words, x_scales, w1, w2, gamma, offs, 
 
         w1_bf = [held.tile([P, 2, P, PACK], BF16, name="w1_bf%d" % u, align_bytes=64) for u in range(2)]
 
-        def cast_w1(engine_copy, c, lo, hi):
-            src = w1_raw[c][:].rearrange("p j (m t) -> p m j t", t=PACK)[:, :, :, lo:hi]
-            dst = w1_bf[lo // 2][:, lo % 2 : lo % 2 + hi - lo, :, 2 * c : 2 * c + 2]
+        def cast_w1(engine_copy, c, lo, hi, cols=slice(0, P)):
+            src = w1_raw[c][:].rearrange("p j (m t) -> p m j t", t=PACK)[:, cols, :, lo:hi]
+            dst = w1_bf[lo // 2][:, lo % 2 : lo % 2 + hi - lo, cols, 2 * c : 2 * c + 2]
             engine_copy(dst.rearrange("p t m j -> p m j t"), src)
 
         cast_w1(nc.scalar.copy, 0, 0, 2)
-        cast_w1(nc.vector.tensor_copy, 0, 2, 4)
+        cast_w1(nc.scalar.copy, 0, 2, 4, slice(0, 48))
+        cast_w1(nc.vector.tensor_copy, 0, 2, 4, slice(48, P))
         cast_w1(nc.vector.tensor_copy, 1, 0, 1)
         cast_w1(nc.vector.tensor_copy, 1, 1, 2)
         cast_w1(nc.scalar.copy, 1, 2, 4)
 
+        w1_codes = held.tile([P, PACK, P], U32, name="w1_codes", align_bytes=64)
+        w1_scales = held.tile([P, PACK, P], U8, name="w1_scales", align_bytes=64)
+        for lo, hi in ((0, 1), (1, 2), (2, 4)):
+            nc.vector.quantize_mx(
+                out=w1_codes[:, lo:hi].rearrange("p t m -> p (t m)").bitcast(FP8X4),
+                scales=w1_scales[:, lo:hi].rearrange("p t m -> p (t m)"),
+                in_=w1_bf[lo // 2][:, lo % 2 : lo % 2 + hi - lo].rearrange("p t m j -> p (t m j)"),
+            )
+
         h = []
         for t in range(PACK):
-            codes = held.tile([P, P], U32, name="w1_codes%d" % t, align_bytes=64)
-            scales = held.tile([P, P], U8, name="w1_scales%d" % t, align_bytes=64)
-            nc.vector.quantize_mx(
-                out=codes[:].bitcast(FP8X4),
-                scales=scales[:],
-                in_=w1_bf[t // 2][:, t % 2].rearrange("p m j -> p (m j)"),
-            )
             banks = []
             for s in range(2):
                 bank = psum.tile([P, HALF], F32, name="h%d_%d" % (t, s), tag="bank%d" % (2 * t + s))
                 nc.tensor.matmul_mx(
                     out=bank[:],
-                    lhsT=codes[:].bitcast(FP8X4),
-                    lhsT_scale=scales[:],
+                    lhsT=w1_codes[:, t, :].bitcast(FP8X4),
+                    lhsT_scale=w1_scales[:, t, :],
                     rhs=x_codes[:, s * HALF : (s + 1) * HALF].bitcast(FP4X4),
                     rhs_scale=x_sc[:, s * HALF : (s + 1) * HALF],
                     start=True,

@@ -20,6 +20,10 @@ ALU = mybir.AluOpType
 P = 128
 PACK = 4
 HALF = S // 2
+QUARTER = S // 4
+LAST = PACK - 1
+SCALAR_CAST_COLS = 48
+SCALAR_WEAVE_END = 448
 
 
 def tile_picked_inorm_relu_p_kernel(tc, x_words, x_scales, w1, w2, gamma, offs, out):
@@ -68,8 +72,8 @@ def tile_picked_inorm_relu_p_kernel(tc, x_words, x_scales, w1, w2, gamma, offs, 
             engine_copy(dst.rearrange("p t m j -> p m j t"), src)
 
         cast_w1(nc.scalar.copy, 0, 0, 2)
-        cast_w1(nc.scalar.copy, 0, 2, 4, slice(0, 48))
-        cast_w1(nc.vector.tensor_copy, 0, 2, 4, slice(48, P))
+        cast_w1(nc.scalar.copy, 0, 2, 4, slice(0, SCALAR_CAST_COLS))
+        cast_w1(nc.vector.tensor_copy, 0, 2, 4, slice(SCALAR_CAST_COLS, P))
         cast_w1(nc.vector.tensor_copy, 1, 0, 1)
         cast_w1(nc.vector.tensor_copy, 1, 1, 2)
         cast_w1(nc.scalar.copy, 1, 2, 4)
@@ -102,8 +106,8 @@ def tile_picked_inorm_relu_p_kernel(tc, x_words, x_scales, w1, w2, gamma, offs, 
 
         neg_gam = held.tile([P, PACK], F32, name="neg_gam")
         nc.scalar.activation(neg_gam[:], gam[:], ACT.Copy, scale=-1.0)
-        gc = held.tile([P, PACK, 2], F32, name="gc")
-        nc.scalar.copy(gc[:, :, 0], gam[:])
+        unscaled = held.tile([P, PACK, 2], F32, name="unscaled")
+        nc.scalar.copy(unscaled[:, :, 0], gam[:])
         w2_bf = held.tile([P, N, PACK], BF16, name="w2_bf", tag="w1_raw1", align_bytes=64)
         nc.scalar.copy(
             w2_bf[:].rearrange("p (c i) j -> p c j i", i=4),
@@ -111,75 +115,84 @@ def tile_picked_inorm_relu_p_kernel(tc, x_words, x_scales, w1, w2, gamma, offs, 
         )
         w2_scales = held.tile([P, N], U8, name="w2_scales", align_bytes=64)
 
-        planes = [held.tile([P, PACK, HALF], BF16, name="planes%d" % s, align_bytes=64) for s in range(2)]
+        stats01 = held.tile([P, 2, 2, 6], F32, name="stats01")
+        stats2 = held.tile([P, 2, 6], F32, name="stats2", tag="stats_then_w2", align_bytes=64)
+        stats3 = held.tile([P, 2, 6], F32, name="stats3")
+        stats = [stats01[:, 0], stats01[:, 1], stats2[:], stats3[:]]
+        early = held.tile([P, 2, QUARTER], F32, name="early", align_bytes=64)
+        rstd = held.tile([P, PACK], F32, name="rstd")
         coef = []
-        early = held.tile([P, 4, 6], F32, name="stats01")
-        third = held.tile([P, 2, 6], F32, name="stats2", tag="stats_then_w2", align_bytes=64)
-        last = held.tile([P, 2, 6], F32, name="stats3")
-        rows = [(0, 1), (2, 3), (0, 1), (0, 1)]
         for t in range(PACK):
-            stats = [early, early, third, last][t]
-            rstd = held.tile([P, 1], F32, name="rstd%d" % t)
             for s in range(2):
-                nc.vector.bn_stats(stats[:, rows[t][s], :], h[t][s][:])
-            first = min(rows[t])
-            nc.vector.bn_aggr(moments[:, t, :], stats[:, first : first + 2, :].rearrange("p s v -> p (s v)"))
-            nc.scalar.activation(rstd[:], moments[:, t, 1:2], ACT.Abs_reciprocal_sqrt, bias=EPS)
-            if t != 2:
-                ab = held.tile([P, 2], F32, name="ab%d" % t)
-                nc.scalar.activation(gc[:, t, 1:2], moments[:, t, 0:1], ACT.Copy, scale=neg_gam[:, t : t + 1])
-                nc.scalar.activation(ab[:], gc[:, t, :], ACT.Copy, scale=rstd[:])
-            else:
-                ab = held.tile([P, 1], F32, name="ab%d" % t)
-                nc.scalar.activation(ab[:], gam[:, t : t + 1], ACT.Copy, scale=rstd[:])
-            coef.append(ab)
-
-        def norm_scalar(t, s, lo=0, hi=HALF):
-            ab = coef[t]
-            nc.scalar.activation(
-                planes[s][:, t, lo:hi], h[t][s][:, lo:hi], ACT.Identity, bias=ab[:, 1:2], scale=ab[:, 0:1]
-            )
-
-        def norm_vector(t, s, lo, hi):
-            nc.vector.tensor_scalar(
-                planes[s][:, t, lo:hi], h[t][s][:, lo:hi], moments[:, t, 0:1], coef[t][:, 0:1], ALU.subtract, ALU.mult
-            )
-
-        for t in range(2):
-            for s in range(2):
-                norm_scalar(t, s)
-        norm_vector(2, 0, 0, HALF)
-        norm_vector(2, 1, 0, HALF)
-        norm_scalar(3, 1, 0, HALF // 2)
-        norm_scalar(3, 1, HALF // 2, HALF)
-        norm_vector(3, 0, 0, HALF // 2)
-        norm_vector(3, 0, HALF // 2, HALF)
+                nc.vector.bn_stats(stats[t][:, s, :], h[t][s][:])
+            nc.vector.bn_aggr(moments[:, t, :], stats[t].rearrange("p s v -> p (s v)"))
+            nc.scalar.activation(rstd[:, t : t + 1], moments[:, t, 1:2], ACT.Abs_reciprocal_sqrt, bias=EPS)
+            nc.scalar.activation(unscaled[:, t, 1:2], moments[:, t, 0:1], ACT.Copy, scale=neg_gam[:, t : t + 1])
+            scale_bias = held.tile([P, 2], F32, name="scale_bias%d" % t)
+            nc.scalar.activation(scale_bias[:], unscaled[:, t, :], ACT.Copy, scale=rstd[:, t : t + 1])
+            coef.append(scale_bias)
+        for s in range(2):
+            nc.scalar.activation(early[:, s, :], h[LAST][s][:, 0:QUARTER], ACT.Copy, scale=gam[:, LAST : LAST + 1])
 
         w2_codes = held.tile([P, N], U32, name="w2_codes", tag="stats_then_w2", align_bytes=64)
         nc.vector.quantize_mx(
             out=w2_codes[:].bitcast(FP8X4), scales=w2_scales[:], in_=w2_bf[:].rearrange("p n j -> p (n j)")
         )
 
-        chunks = [(0, 128), (128, 256), (256, 384), (384, 512)]
-        z_bf = [held.tile([P, hi - lo, PACK], BF16, name="z_bf%d" % lo, align_bytes=64) for lo, hi in chunks]
+        normed = held.tile([P, 2, PACK, HALF], BF16, name="normed", align_bytes=64)
 
-        def weave(c, lo, hi, on_scalar):
-            base = chunks[c][0]
-            dst = z_bf[c][:, lo - base : hi - base, :].rearrange("p (g i) t -> p g t i", i=4)
-            src = planes[lo // HALF][:, :, lo % HALF : lo % HALF + hi - lo].rearrange("p t (g i) -> p g t i", i=4)
-            if on_scalar:
-                nc.scalar.activation(dst, src, ACT.Relu)
-            else:
-                nc.vector.tensor_scalar_max(dst, src, 0.0)
+        def norm_scalar(t, s, lo=0, hi=HALF):
+            nc.scalar.activation(
+                normed[:, s, t, lo:hi], h[t][s][:, lo:hi], ACT.Identity, bias=coef[t][:, 1:2], scale=coef[t][:, 0:1]
+            )
+
+        def norm_vector(t, s, lo=0, hi=HALF):
+            nc.vector.tensor_scalar(
+                normed[:, s, t, lo:hi], h[t][s][:, lo:hi], moments[:, t, 0:1], coef[t][:, 0:1], ALU.subtract, ALU.mult
+            )
+
+        for s in range(2):
+            nc.vector.tensor_scalar(
+                normed[:, s, LAST, 0:QUARTER],
+                early[:, s, :],
+                unscaled[:, LAST, 1:2],
+                rstd[:, LAST : LAST + 1],
+                ALU.add,
+                ALU.mult,
+            )
+        norm_vector(LAST, 0, QUARTER, HALF)
+        norm_scalar(0, 0)
+        norm_scalar(0, 1)
+        norm_scalar(1, 0, 0, QUARTER)
+        norm_scalar(1, 0, QUARTER, HALF)
+        norm_vector(2, 0)
+        norm_vector(1, 1)
+        norm_scalar(LAST, 1, QUARTER, HALF)
+        norm_scalar(2, 1, 0, QUARTER)
+        norm_scalar(2, 1, QUARTER, HALF)
+
+        z_bf = [held.tile([P, QUARTER, PACK], BF16, name="z_bf%d" % c, align_bytes=64) for c in range(4)]
+
+        def weave_views(lo, hi):
+            dst = z_bf[lo // QUARTER][:, lo % QUARTER : lo % QUARTER + hi - lo, :]
+            src = normed[:, lo // HALF, :, lo % HALF : lo % HALF + hi - lo]
+            return dst.rearrange("p (g i) t -> p g t i", i=4), src.rearrange("p t (g i) -> p g t i", i=4)
+
+        def weave_vector(lo, hi):
+            dst, src = weave_views(lo, hi)
+            nc.vector.tensor_scalar_max(dst, src, 0.0)
+
+        def weave_scalar(lo, hi):
+            dst, src = weave_views(lo, hi)
+            nc.scalar.activation(dst, src, ACT.Relu)
 
         def second_layer(c, engine_copy, queue):
-            lo, hi = chunks[c]
-            z_codes = held.tile([P, hi - lo], U32, name="z_codes%d" % c, align_bytes=64)
-            z_scales = held.tile([P, hi - lo], U8, name="z_scales%d" % c, align_bytes=64)
+            z_codes = held.tile([P, QUARTER], U32, name="z_codes%d" % c, align_bytes=64)
+            z_scales = held.tile([P, QUARTER], U8, name="z_scales%d" % c, align_bytes=64)
             nc.vector.quantize_mx(
                 out=z_codes[:].bitcast(FP8X4), scales=z_scales[:], in_=z_bf[c][:].rearrange("p n t -> p (n t)")
             )
-            acc = psum.tile([P, hi - lo], F32, name="acc%d" % c, tag="bank%d" % c)
+            acc = psum.tile([P, QUARTER], F32, name="acc%d" % c, tag="bank%d" % c)
             nc.tensor.matmul_mx(
                 out=acc[:],
                 lhsT=w2_codes[:].bitcast(FP8X4),
@@ -189,16 +202,16 @@ def tile_picked_inorm_relu_p_kernel(tc, x_words, x_scales, w1, w2, gamma, offs, 
                 start=True,
                 stop=True,
             )
-            result = held.tile([P, hi - lo], F32, name="result%d" % c)
+            result = held.tile([P, QUARTER], F32, name="result%d" % c)
             engine_copy(result[:], acc[:])
-            queue.dma_start(out=out[:, lo:hi], in_=result[:])
+            queue.dma_start(out=out[:, c * QUARTER : (c + 1) * QUARTER], in_=result[:])
 
-        weave(0, 0, 128, False)
-        weave(1, 128, 256, False)
-        weave(2, 256, 384, True)
-        weave(3, 384, 448, True)
+        weave_vector(0, QUARTER)
+        weave_vector(QUARTER, HALF)
+        weave_scalar(HALF, HALF + QUARTER)
+        weave_scalar(HALF + QUARTER, SCALAR_WEAVE_END)
         second_layer(0, nc.scalar.copy, nc.sync)
-        weave(3, 448, 512, False)
+        weave_vector(SCALAR_WEAVE_END, S)
         second_layer(1, nc.scalar.copy, nc.sync)
         second_layer(2, nc.scalar.copy, nc.scalar)
         second_layer(3, nc.vector.tensor_copy, nc.sync)

@@ -23,6 +23,8 @@ HALF = S // 2
 QUARTER = S // 4
 LAST = PACK - 1
 SCALAR_CAST_COLS = 48
+FIRST_CAST_COLS = 80
+LATE_CAST_COLS = 96
 SCALAR_WEAVE_END = 448
 
 
@@ -33,7 +35,7 @@ def tile_picked_inorm_relu_p_kernel(tc, x_words, x_scales, w1, w2, gamma, offs, 
         psum = ctx.enter_context(tc.psum_pool(name="psum", bufs=1))
 
         offsets = held.tile([P, S // 16], U16, name="offsets")
-        word_table = held.tile([P, T], U16, name="word_table", tag="words_then_w2", align_bytes=64)
+        word_table = held.tile([P, T], U16, name="word_table", align_bytes=64)
         scale_table = held.tile([P, T], U8, name="scale_table", align_bytes=64)
         w1_raw = [held.tile([P, 2, H], F32, name="w1_raw%d" % c, tag="w1_raw%d" % c, align_bytes=64) for c in range(2)]
         warm_in = held.tile([P, 1], F32, name="warm_in", tag="warm_then_gamma")
@@ -53,30 +55,36 @@ def tile_picked_inorm_relu_p_kernel(tc, x_words, x_scales, w1, w2, gamma, offs, 
         w1_rows = w1.rearrange("(p j) c -> p j c", j=PACK)
         for c in range(2):
             nc.sync.dma_start(out=w1_raw[c][:], in_=w1_rows[:, 2 * c : 2 * c + 2, :])
-        gam = held.tile([P, PACK], F32, name="gam", tag="warm_then_gamma")
-        nc.sync.dma_start(out=gam[:], in_=gamma.rearrange("(p t) o -> p (t o)", t=PACK))
+        w2_raw = held.tile([P, PACK, N], F32, name="w2_raw", align_bytes=64)
+        w2_dealt = w2.rearrange("(a t r) n -> r a t n", t=PACK, r=2)
+        for r in range(2):
+            nc.sync.dma_start(out=w2_raw[r:P:2], in_=w2_dealt[r])
+        gam_run = held.tile([P, 2 * PACK - 1], F32, name="gam_run", tag="warm_then_gamma")
+        gamma_rows = gamma.rearrange("(a e) o -> a (e o)", e=2 * PACK)
+        for r in range(2):
+            nc.sync.dma_start(out=gam_run[r:P:2, :], in_=gamma_rows[:, r : r + 2 * PACK - 1])
+        gam = gam_run[:, 0 : 2 * PACK - 1 : 2]
 
         x_codes = held.tile([P, S], U16, name="x_codes", align_bytes=64)
         x_sc = held.tile([P, S], U8, name="x_sc", align_bytes=64)
         nc.vector.tensor_copy(x_codes[:], word_table[:].indirect(offsets[:]))
         nc.vector.tensor_copy(x_sc[:], scale_table[:].indirect(offsets[:]))
 
-        w2_raw = held.tile([P, PACK, N], F32, name="w2_raw", tag="words_then_w2", align_bytes=64)
-        nc.sync.dma_start(out=w2_raw[:], in_=w2.rearrange("(p j) n -> p j n", j=PACK))
-
         w1_bf = [held.tile([P, 2, P, PACK], BF16, name="w1_bf%d" % u, align_bytes=64) for u in range(2)]
 
-        def cast_w1(engine_copy, c, lo, hi, cols=slice(0, P)):
-            src = w1_raw[c][:].rearrange("p j (m t) -> p m j t", t=PACK)[:, cols, :, lo:hi]
-            dst = w1_bf[lo // 2][:, lo % 2 : lo % 2 + hi - lo, cols, 2 * c : 2 * c + 2]
-            engine_copy(dst.rearrange("p t m j -> p m j t"), src)
+        def cast_w1(engine_copy, c, lo, hi, first=0, last=P):
+            src = w1_raw[c][:].rearrange("p j (a t r) -> p a j t r", t=PACK, r=2)[:, first // 2 : last // 2, :, lo:hi]
+            dst = w1_bf[lo // 2][:, lo % 2 : lo % 2 + hi - lo, first:last, 2 * c : 2 * c + 2]
+            engine_copy(dst.rearrange("p t (a r) j -> p a j t r", r=2), src)
 
         cast_w1(nc.scalar.copy, 0, 0, 2)
-        cast_w1(nc.scalar.copy, 0, 2, 4, slice(0, SCALAR_CAST_COLS))
-        cast_w1(nc.vector.tensor_copy, 0, 2, 4, slice(SCALAR_CAST_COLS, P))
-        cast_w1(nc.vector.tensor_copy, 1, 0, 1)
+        cast_w1(nc.scalar.copy, 0, 2, 4, 0, SCALAR_CAST_COLS)
+        cast_w1(nc.vector.tensor_copy, 0, 2, 4, SCALAR_CAST_COLS, P)
+        cast_w1(nc.vector.tensor_copy, 1, 0, 1, 0, FIRST_CAST_COLS)
+        cast_w1(nc.scalar.copy, 1, 0, 1, FIRST_CAST_COLS, P)
         cast_w1(nc.vector.tensor_copy, 1, 1, 2)
-        cast_w1(nc.scalar.copy, 1, 2, 4)
+        cast_w1(nc.scalar.copy, 1, 2, 4, 0, LATE_CAST_COLS)
+        cast_w1(nc.vector.tensor_copy, 1, 2, 4, LATE_CAST_COLS, P)
 
         w1_codes = held.tile([P, PACK, P], U32, name="w1_codes", align_bytes=64)
         w1_scales = held.tile([P, PACK, P], U8, name="w1_scales", align_bytes=64)
@@ -105,9 +113,9 @@ def tile_picked_inorm_relu_p_kernel(tc, x_words, x_scales, w1, w2, gamma, offs, 
             h.append(banks)
 
         neg_gam = held.tile([P, PACK], F32, name="neg_gam")
-        nc.scalar.activation(neg_gam[:], gam[:], ACT.Copy, scale=-1.0)
+        nc.scalar.activation(neg_gam[:], gam, ACT.Copy, scale=-1.0)
         unscaled = held.tile([P, PACK, 2], F32, name="unscaled")
-        nc.scalar.copy(unscaled[:, :, 0], gam[:])
+        nc.scalar.copy(unscaled[:, :, 0], gam)
         w2_bf = held.tile([P, N, PACK], BF16, name="w2_bf", tag="w1_raw1", align_bytes=64)
         nc.scalar.copy(
             w2_bf[:].rearrange("p (c i) j -> p c j i", i=4),
@@ -115,31 +123,57 @@ def tile_picked_inorm_relu_p_kernel(tc, x_words, x_scales, w1, w2, gamma, offs, 
         )
         w2_scales = held.tile([P, N], U8, name="w2_scales", align_bytes=64)
 
-        stats01 = held.tile([P, 2, 2, 6], F32, name="stats01")
-        stats2 = held.tile([P, 2, 6], F32, name="stats2", tag="stats_then_w2", align_bytes=64)
-        stats3 = held.tile([P, 2, 6], F32, name="stats3")
-        stats = [stats01[:, 0], stats01[:, 1], stats2[:], stats3[:]]
-        early = held.tile([P, 2, QUARTER], F32, name="early", align_bytes=64)
+        stats = [
+            held.tile([P, 2, 6], F32, name="stats%d" % t, tag="stats%d" % t, align_bytes=64) for t in range(PACK)
+        ]
         rstd = held.tile([P, PACK], F32, name="rstd")
-        coef = []
-        for t in range(PACK):
-            for s in range(2):
-                nc.vector.bn_stats(stats[t][:, s, :], h[t][s][:])
-            nc.vector.bn_aggr(moments[:, t, :], stats[t].rearrange("p s v -> p (s v)"))
-            nc.scalar.activation(rstd[:, t : t + 1], moments[:, t, 1:2], ACT.Abs_reciprocal_sqrt, bias=EPS)
-            nc.scalar.activation(unscaled[:, t, 1:2], moments[:, t, 0:1], ACT.Copy, scale=neg_gam[:, t : t + 1])
-            scale_bias = held.tile([P, 2], F32, name="scale_bias%d" % t)
-            nc.scalar.activation(scale_bias[:], unscaled[:, t, :], ACT.Copy, scale=rstd[:, t : t + 1])
-            coef.append(scale_bias)
-        for s in range(2):
-            nc.scalar.activation(early[:, s, :], h[LAST][s][:, 0:QUARTER], ACT.Copy, scale=gam[:, LAST : LAST + 1])
-
-        w2_codes = held.tile([P, N], U32, name="w2_codes", tag="stats_then_w2", align_bytes=64)
-        nc.vector.quantize_mx(
-            out=w2_codes[:].bitcast(FP8X4), scales=w2_scales[:], in_=w2_bf[:].rearrange("p n j -> p (n j)")
-        )
-
+        coef = [held.tile([P, 2], F32, name="coef%d" % t) for t in range(PACK)]
+        early = [
+            held.tile([P, 2, HALF], F32, name="early%d" % t, tag="early%d" % t, align_bytes=64) for t in range(PACK)
+        ]
         normed = held.tile([P, 2, PACK, HALF], BF16, name="normed", align_bytes=64)
+        w2q = []
+
+        def stat(t, s):
+            nc.vector.bn_stats(stats[t][:, s, :], h[t][s][:])
+
+        def aggr(t):
+            nc.vector.bn_aggr(moments[:, t, :], stats[t][:].rearrange("p s v -> p (s v)"))
+
+        def inv_dev(t):
+            nc.scalar.activation(rstd[:, t : t + 1], moments[:, t, 1:2], ACT.Abs_reciprocal_sqrt, bias=EPS)
+
+        def shift(t):
+            nc.scalar.activation(unscaled[:, t, 1:2], moments[:, t, 0:1], ACT.Copy, scale=neg_gam[:, t : t + 1])
+
+        def scale_bias(t):
+            nc.scalar.activation(coef[t][:], unscaled[:, t, :], ACT.Copy, scale=rstd[:, t : t + 1])
+
+        def scale_only(t):
+            nc.scalar.activation(coef[t][:, 0:1], unscaled[:, t, 0:1], ACT.Copy, scale=rstd[:, t : t + 1])
+
+        def scale_vector(t):
+            nc.vector.tensor_scalar_mul(coef[t][:, 0:1], rstd[:, t : t + 1], unscaled[:, t, 0:1])
+
+        def copy_early(t, s, lo=0, hi=HALF):
+            nc.scalar.activation(early[t][:, s, lo:hi], h[t][s][:, lo:hi], ACT.Copy, scale=gam_run[:, 2 * t : 2 * t + 1])
+
+        def finish(engine, t, s, lo=0, hi=HALF):
+            engine.tensor_scalar(
+                normed[:, s, t, lo:hi], early[t][:, s, lo:hi], unscaled[:, t, 1:2], rstd[:, t : t + 1], ALU.add, ALU.mult
+            )
+
+        def finish_plane(engine, t):
+            engine.tensor_scalar(
+                normed[:, :, t, :], early[t][:], unscaled[:, t, 1:2], rstd[:, t : t + 1], ALU.add, ALU.mult
+            )
+
+        def quantise_w2(tag):
+            codes = held.tile([P, N], U32, name="w2_codes", tag=tag, align_bytes=64)
+            nc.vector.quantize_mx(
+                out=codes[:].bitcast(FP8X4), scales=w2_scales[:], in_=w2_bf[:].rearrange("p n j -> p (n j)")
+            )
+            w2q.append(codes)
 
         def norm_scalar(t, s, lo=0, hi=HALF):
             nc.scalar.activation(
@@ -151,25 +185,45 @@ def tile_picked_inorm_relu_p_kernel(tc, x_words, x_scales, w1, w2, gamma, offs, 
                 normed[:, s, t, lo:hi], h[t][s][:, lo:hi], moments[:, t, 0:1], coef[t][:, 0:1], ALU.subtract, ALU.mult
             )
 
-        for s in range(2):
-            nc.vector.tensor_scalar(
-                normed[:, s, LAST, 0:QUARTER],
-                early[:, s, :],
-                unscaled[:, LAST, 1:2],
-                rstd[:, LAST : LAST + 1],
-                ALU.add,
-                ALU.mult,
-            )
-        norm_vector(LAST, 0, QUARTER, HALF)
-        norm_scalar(0, 0)
-        norm_scalar(0, 1)
-        norm_scalar(1, 0, 0, QUARTER)
-        norm_scalar(1, 0, QUARTER, HALF)
+        stat(0, 0)
+        copy_early(0, 0)
+        stat(0, 1)
+        copy_early(0, 1)
+        aggr(0)
+        inv_dev(0)
+        shift(0)
+        finish_plane(nc.gpsimd, 0)
+        stat(1, 0)
+        stat(1, 1)
+        aggr(1)
+        inv_dev(1)
+        shift(1)
+        scale_bias(1)
+        stat(2, 0)
+        stat(2, 1)
+        aggr(2)
+        inv_dev(2)
+        shift(2)
+        scale_bias(2)
+        stat(3, 0)
+        stat(3, 1)
+        aggr(3)
+        inv_dev(3)
+        shift(3)
+        scale_bias(3)
+        copy_early(3, 0, 0, QUARTER)
+        copy_early(3, 1, 0, QUARTER)
+        quantise_w2("early0")
+        finish(nc.vector, 3, 0, 0, QUARTER)
+        finish(nc.vector, 3, 1, 0, QUARTER)
+        norm_vector(3, 0, QUARTER, HALF)
+        norm_scalar(1, 0)
+        norm_scalar(1, 1)
         norm_vector(2, 0)
-        norm_vector(1, 1)
-        norm_scalar(LAST, 1, QUARTER, HALF)
+        norm_scalar(3, 1, QUARTER, HALF)
         norm_scalar(2, 1, 0, QUARTER)
         norm_scalar(2, 1, QUARTER, HALF)
+        w2_codes = w2q[0]
 
         z_bf = [held.tile([P, QUARTER, PACK], BF16, name="z_bf%d" % c, align_bytes=64) for c in range(4)]
 

@@ -70,7 +70,7 @@ def tile_picked_inorm_relu_p_kernel(tc, x_words, x_scales, w1, w2, gamma, offs, 
         nc.vector.tensor_copy(x_codes[:], word_table[:].indirect(offsets[:]))
         nc.vector.tensor_copy(x_sc[:], scale_table[:].indirect(offsets[:]))
 
-        w1_bf = [held.tile([P, 2, P, PACK], BF16, name="w1_bf%d" % u, align_bytes=64) for u in range(2)]
+        w1_bf = [held.tile([P, 2, P, PACK], BF16, name="w1_bf%d" % u, tag="w1_bf%d" % u, align_bytes=64) for u in range(2)]
 
         def cast_w1(engine_copy, c, lo, hi, first=0, last=P):
             src = w1_raw[c][:].rearrange("p j (a t r) -> p a j t r", t=PACK, r=2)[:, first // 2 : last // 2, :, lo:hi]
@@ -116,11 +116,8 @@ def tile_picked_inorm_relu_p_kernel(tc, x_words, x_scales, w1, w2, gamma, offs, 
         nc.scalar.activation(neg_gam[:], gam, ACT.Copy, scale=-1.0)
         unscaled = held.tile([P, PACK, 2], F32, name="unscaled")
         nc.scalar.copy(unscaled[:, :, 0], gam)
-        w2_bf = held.tile([P, N, PACK], BF16, name="w2_bf", tag="w1_raw1", align_bytes=64)
-        nc.scalar.copy(
-            w2_bf[:].rearrange("p (c i) j -> p c j i", i=4),
-            w2_raw[:].rearrange("p j (c i) -> p c j i", i=4),
-        )
+        w2_bf = held.tile([P, N, PACK], BF16, name="w2_bf", tag="w1_bf1", align_bytes=64)
+        nc.gpsimd.tensor_scalar(w2_bf[:], w2_raw[:].rearrange("p j n -> p n j"), 1.0, 0.0, ALU.mult, ALU.add)
         w2_scales = held.tile([P, N], U8, name="w2_scales", align_bytes=64)
 
         stats = [

@@ -118,7 +118,6 @@ def tile_picked_inorm_relu_p_kernel(tc, x_words, x_scales, w1, w2, gamma, offs, 
         nc.scalar.copy(unscaled[:, :, 0], gam)
         w2_bf = held.tile([P, N, PACK], BF16, name="w2_bf", tag="w1_bf1", align_bytes=64)
         nc.gpsimd.tensor_scalar(w2_bf[:], w2_raw[:].rearrange("p j n -> p n j"), 1.0, 0.0, ALU.mult, ALU.add)
-        w2_scales = held.tile([P, N], U8, name="w2_scales", align_bytes=64)
 
         stats = [
             held.tile([P, 2, 6], F32, name="stats%d" % t, tag="stats%d" % t, align_bytes=64) for t in range(PACK)
@@ -128,7 +127,7 @@ def tile_picked_inorm_relu_p_kernel(tc, x_words, x_scales, w1, w2, gamma, offs, 
         early = [
             held.tile([P, 2, HALF], F32, name="early%d" % t, tag="early%d" % t, align_bytes=64) for t in range(PACK)
         ]
-        normed = held.tile([P, 2, PACK, HALF], BF16, name="normed", align_bytes=64)
+        normed = held.tile([P, PACK, 2, HALF], BF16, name="normed", align_bytes=64)
         w2q = []
 
         def stat(t, s):
@@ -157,29 +156,35 @@ def tile_picked_inorm_relu_p_kernel(tc, x_words, x_scales, w1, w2, gamma, offs, 
 
         def finish(engine, t, s, lo=0, hi=HALF):
             engine.tensor_scalar(
-                normed[:, s, t, lo:hi], early[t][:, s, lo:hi], unscaled[:, t, 1:2], rstd[:, t : t + 1], ALU.add, ALU.mult
+                normed[:, t, s, lo:hi], early[t][:, s, lo:hi], unscaled[:, t, 1:2], rstd[:, t : t + 1], ALU.add, ALU.mult
             )
 
         def finish_plane(engine, t):
             engine.tensor_scalar(
-                normed[:, :, t, :], early[t][:], unscaled[:, t, 1:2], rstd[:, t : t + 1], ALU.add, ALU.mult
+                normed[:, t], early[t][:], unscaled[:, t, 1:2], rstd[:, t : t + 1], ALU.add, ALU.mult
             )
 
-        def quantise_w2(tag):
-            codes = held.tile([P, N], U32, name="w2_codes", tag=tag, align_bytes=64)
-            nc.vector.quantize_mx(
-                out=codes[:].bitcast(FP8X4), scales=w2_scales[:], in_=w2_bf[:].rearrange("p n j -> p (n j)")
+        def finish_both(engine, t, lo, hi):
+            engine.tensor_scalar(
+                normed[:, t, :, lo:hi], early[t][:, :, lo:hi], unscaled[:, t, 1:2], rstd[:, t : t + 1], ALU.add, ALU.mult
             )
-            w2q.append(codes)
+
+        def quantise_w2(tag, scale_tag):
+            codes = held.tile([P, N], U32, name="w2_codes", tag=tag, align_bytes=64)
+            scales = held.tile([P, N], U8, name="w2_scales", tag=scale_tag, align_bytes=64)
+            nc.vector.quantize_mx(
+                out=codes[:].bitcast(FP8X4), scales=scales[:], in_=w2_bf[:].rearrange("p n j -> p (n j)")
+            )
+            w2q.extend([codes, scales])
 
         def norm_scalar(t, s, lo=0, hi=HALF):
             nc.scalar.activation(
-                normed[:, s, t, lo:hi], h[t][s][:, lo:hi], ACT.Identity, bias=coef[t][:, 1:2], scale=coef[t][:, 0:1]
+                normed[:, t, s, lo:hi], h[t][s][:, lo:hi], ACT.Identity, bias=coef[t][:, 1:2], scale=coef[t][:, 0:1]
             )
 
         def norm_vector(t, s, lo=0, hi=HALF):
             nc.vector.tensor_scalar(
-                normed[:, s, t, lo:hi], h[t][s][:, lo:hi], moments[:, t, 0:1], coef[t][:, 0:1], ALU.subtract, ALU.mult
+                normed[:, t, s, lo:hi], h[t][s][:, lo:hi], moments[:, t, 0:1], coef[t][:, 0:1], ALU.subtract, ALU.mult
             )
 
         stat(0, 0)
@@ -210,7 +215,7 @@ def tile_picked_inorm_relu_p_kernel(tc, x_words, x_scales, w1, w2, gamma, offs, 
         scale_bias(3)
         copy_early(3, 0, 0, QUARTER)
         copy_early(3, 1, 0, QUARTER)
-        quantise_w2("early0")
+        quantise_w2("early0", "w2s")
         finish(nc.vector, 3, 0, 0, QUARTER)
         finish(nc.vector, 3, 1, 0, QUARTER)
         norm_vector(3, 0, QUARTER, HALF)
@@ -220,14 +225,17 @@ def tile_picked_inorm_relu_p_kernel(tc, x_words, x_scales, w1, w2, gamma, offs, 
         norm_scalar(3, 1, QUARTER, HALF)
         norm_scalar(2, 1, 0, QUARTER)
         norm_scalar(2, 1, QUARTER, HALF)
-        w2_codes = w2q[0]
+        w2_codes, w2_scales = w2q
 
-        z_bf = [held.tile([P, QUARTER, PACK], BF16, name="z_bf%d" % c, align_bytes=64) for c in range(4)]
+        z_bf = held.tile([P, S, PACK], BF16, name="z_bf", align_bytes=64)
+        z_codes = held.tile([P, S], U32, name="z_codes", align_bytes=64)
+        z_scales = held.tile([P, S], U8, name="z_scales", align_bytes=64)
+        result = held.tile([P, S], F32, name="result", align_bytes=64)
+        planes = normed[:].rearrange("p t s n -> p t (s n)")
 
         def weave_views(lo, hi):
-            dst = z_bf[lo // QUARTER][:, lo % QUARTER : lo % QUARTER + hi - lo, :]
-            src = normed[:, lo // HALF, :, lo % HALF : lo % HALF + hi - lo]
-            return dst.rearrange("p (g i) t -> p g t i", i=4), src.rearrange("p t (g i) -> p g t i", i=4)
+            dst = z_bf[:, lo:hi, :].rearrange("p (g i) t -> p g t i", i=4)
+            return dst, planes[:, :, lo:hi].rearrange("p t (g i) -> p g t i", i=4)
 
         def weave_vector(lo, hi):
             dst, src = weave_views(lo, hi)
@@ -237,32 +245,45 @@ def tile_picked_inorm_relu_p_kernel(tc, x_words, x_scales, w1, w2, gamma, offs, 
             dst, src = weave_views(lo, hi)
             nc.scalar.activation(dst, src, ACT.Relu)
 
-        def second_layer(c, engine_copy, queue):
-            z_codes = held.tile([P, QUARTER], U32, name="z_codes%d" % c, align_bytes=64)
-            z_scales = held.tile([P, QUARTER], U8, name="z_scales%d" % c, align_bytes=64)
+        def quantise_z(lo, hi):
             nc.vector.quantize_mx(
-                out=z_codes[:].bitcast(FP8X4), scales=z_scales[:], in_=z_bf[c][:].rearrange("p n t -> p (n t)")
+                out=z_codes[:, lo:hi].bitcast(FP8X4),
+                scales=z_scales[:, lo:hi],
+                in_=z_bf[:, lo:hi, :].rearrange("p n t -> p (n t)"),
             )
-            acc = psum.tile([P, QUARTER], F32, name="acc%d" % c, tag="bank%d" % c)
+
+        def second_layer(lo, hi, bank, engine_copy):
+            acc = psum.tile([P, hi - lo], F32, name="acc%d" % bank, tag="bank%d" % bank)
             nc.tensor.matmul_mx(
                 out=acc[:],
                 lhsT=w2_codes[:].bitcast(FP8X4),
                 lhsT_scale=w2_scales[:],
-                rhs=z_codes[:].bitcast(FP8X4),
-                rhs_scale=z_scales[:],
+                rhs=z_codes[:, lo:hi].bitcast(FP8X4),
+                rhs_scale=z_scales[:, lo:hi],
                 start=True,
                 stop=True,
             )
-            result = held.tile([P, QUARTER], F32, name="result%d" % c)
-            engine_copy(result[:], acc[:])
-            queue.dma_start(out=out[:, c * QUARTER : (c + 1) * QUARTER], in_=result[:])
+            engine_copy(result[:, lo:hi], acc[:])
 
-        weave_vector(0, QUARTER)
-        weave_vector(QUARTER, HALF)
-        weave_scalar(HALF, HALF + QUARTER)
-        weave_scalar(HALF + QUARTER, SCALAR_WEAVE_END)
-        second_layer(0, nc.scalar.copy, nc.sync)
-        weave_vector(SCALAR_WEAVE_END, S)
-        second_layer(1, nc.scalar.copy, nc.sync)
-        second_layer(2, nc.scalar.copy, nc.scalar)
-        second_layer(3, nc.vector.tensor_copy, nc.sync)
+        def store(lo, hi, queue):
+            queue.dma_start(out=out[:, lo:hi], in_=result[:, lo:hi])
+
+        weave_vector(0, 128)
+        weave_vector(128, 256)
+        weave_scalar(256, 384)
+        weave_scalar(384, 448)
+        quantise_z(0, 128)
+        second_layer(0, 128, 0, nc.scalar.copy)
+        store(0, 128, nc.sync)
+        weave_vector(448, 512)
+        quantise_z(128, 256)
+        second_layer(128, 256, 1, nc.scalar.copy)
+        store(128, 256, nc.sync)
+        quantise_z(256, 384)
+        second_layer(256, 384, 2, nc.scalar.copy)
+        store(256, 384, nc.scalar)
+        quantise_z(448, 512)
+        second_layer(448, 512, 4, nc.scalar.copy)
+        quantise_z(384, 448)
+        second_layer(384, 448, 3, nc.vector.tensor_copy)
+        store(384, 512, nc.sync)

@@ -42,7 +42,7 @@ def tile_picked_inorm_relu_p_kernel(tc, x_words, x_scales, w1, w2, gamma, offs, 
         warm_out = held.tile([P, 1], F32, name="warm_out")
 
         nc.gpsimd.memset(scale_table[:].bitcast(I32), 0)
-        nc.vector.memset(warm_in[:], 1.0)
+        nc.gpsimd.memset(warm_in[:], 1.0)
         moments = held.tile([P, PACK, 2], F32, name="moments")
         nc.sync.dma_start(offsets[:], offs)
         nc.scalar.dma_start(out=word_table[:].bitcast(I32), in_=x_words[0].bitcast(I32))
@@ -199,8 +199,7 @@ def tile_picked_inorm_relu_p_kernel(tc, x_words, x_scales, w1, w2, gamma, offs, 
         stat(1, 1)
         aggr(1)
         inv_dev(1)
-        shift(1)
-        scale_bias(1)
+        scale_only(1)
         stat(2, 0)
         stat(2, 1)
         aggr(2)
@@ -215,16 +214,15 @@ def tile_picked_inorm_relu_p_kernel(tc, x_words, x_scales, w1, w2, gamma, offs, 
         scale_bias(3)
         copy_early(3, 0, 0, QUARTER)
         copy_early(3, 1, 0, QUARTER)
+        norm_vector(1, 0)
+        norm_vector(1, 1)
         quantise_w2("early0", "w2s")
         finish(nc.vector, 3, 0, 0, QUARTER)
         finish(nc.vector, 3, 1, 0, QUARTER)
         norm_vector(3, 0, QUARTER, HALF)
-        norm_scalar(1, 0)
-        norm_scalar(1, 1)
-        norm_vector(2, 0)
+        norm_scalar(2, 0)
+        norm_scalar(2, 1)
         norm_scalar(3, 1, QUARTER, HALF)
-        norm_scalar(2, 1, 0, QUARTER)
-        norm_scalar(2, 1, QUARTER, HALF)
         w2_codes, w2_scales = w2q
 
         z_bf = held.tile([P, S, PACK], BF16, name="z_bf", align_bytes=64)
@@ -271,11 +269,11 @@ def tile_picked_inorm_relu_p_kernel(tc, x_words, x_scales, w1, w2, gamma, offs, 
         weave_vector(0, 128)
         weave_vector(128, 256)
         weave_scalar(256, 384)
-        weave_scalar(384, 448)
+        weave_scalar(384, 440)
         quantise_z(0, 128)
         second_layer(0, 128, 0, nc.scalar.copy)
         store(0, 128, nc.sync)
-        weave_vector(448, 512)
+        weave_vector(440, 512)
         quantise_z(128, 256)
         second_layer(128, 256, 1, nc.scalar.copy)
         store(128, 256, nc.sync)

@@ -62,7 +62,7 @@ def tile_picked_inorm_relu_p_kernel(tc, x_words, x_scales, w1, w2, gamma, offs, 
         gam_run = held.tile([P, 2 * PACK - 1], F32, name="gam_run", tag="warm_then_gamma")
         gamma_rows = gamma.rearrange("(a e) o -> a (e o)", e=2 * PACK)
         for r in range(2):
-            nc.sync.dma_start(out=gam_run[r:P:2, :], in_=gamma_rows[:, r : r + 2 * PACK - 1])
+            nc.scalar.dma_start(out=gam_run[r:P:2, :], in_=gamma_rows[:, r : r + 2 * PACK - 1])
         gam = gam_run[:, 0 : 2 * PACK - 1 : 2]
 
         x_codes = held.tile([P, S], U16, name="x_codes", align_bytes=64)
@@ -197,15 +197,19 @@ def tile_picked_inorm_relu_p_kernel(tc, x_words, x_scales, w1, w2, gamma, offs, 
         finish_plane(nc.gpsimd, 0)
         stat(1, 0)
         stat(1, 1)
+        copy_early(1, 1)
         aggr(1)
         inv_dev(1)
+        shift(1)
+        finish(nc.gpsimd, 1, 1)
         scale_only(1)
         stat(2, 0)
+        copy_early(2, 0)
         stat(2, 1)
+        copy_early(2, 1)
         aggr(2)
         inv_dev(2)
         shift(2)
-        scale_bias(2)
         stat(3, 0)
         stat(3, 1)
         aggr(3)
@@ -215,13 +219,11 @@ def tile_picked_inorm_relu_p_kernel(tc, x_words, x_scales, w1, w2, gamma, offs, 
         copy_early(3, 0, 0, QUARTER)
         copy_early(3, 1, 0, QUARTER)
         norm_vector(1, 0)
-        norm_vector(1, 1)
-        quantise_w2("early0", "w2s")
+        quantise_w2("early1", "w2s")
+        finish_plane(nc.vector, 2)
         finish(nc.vector, 3, 0, 0, QUARTER)
         finish(nc.vector, 3, 1, 0, QUARTER)
         norm_vector(3, 0, QUARTER, HALF)
-        norm_scalar(2, 0)
-        norm_scalar(2, 1)
         norm_scalar(3, 1, QUARTER, HALF)
         w2_codes, w2_scales = w2q
 
@@ -269,11 +271,11 @@ def tile_picked_inorm_relu_p_kernel(tc, x_words, x_scales, w1, w2, gamma, offs, 
         weave_vector(0, 128)
         weave_vector(128, 256)
         weave_scalar(256, 384)
-        weave_scalar(384, 440)
+        weave_scalar(384, 448)
         quantise_z(0, 128)
         second_layer(0, 128, 0, nc.scalar.copy)
         store(0, 128, nc.sync)
-        weave_vector(440, 512)
+        weave_vector(448, 512)
         quantise_z(128, 256)
         second_layer(128, 256, 1, nc.scalar.copy)
         store(128, 256, nc.sync)

from contextlib import ExitStack

import concourse.mybir as mybir

K, T, S, H, N = 512, 1024, 512, 512, 128
FLOPS = 2 * K * H * S + 2 * H * N * S
EPS = 1e-5

F32 = mybir.dt.float32
BF16 = mybir.dt.bfloat16
I32 = mybir.dt.int32
U32 = mybir.dt.uint32
U16 = mybir.dt.uint16
U8 = mybir.dt.uint8
FP8X4 = mybir.dt.float8_e4m3fn_x4
FP4X4 = mybir.dt.float4_e2m1fn_x4
ACT = mybir.ActivationFunctionType
ALU = mybir.AluOpType

P = 128
PACK = 4
HALF = S // 2
QUARTER = S // 4
LAST = PACK - 1
SCALAR_CAST_COLS = 48
FIRST_CAST_COLS = 80
LATE_CAST_COLS = 96
SCALAR_WEAVE_END = 448


def tile_picked_inorm_relu_p_kernel(tc, x_words, x_scales, w1, w2, gamma, offs, out):
    nc = tc.nc
    with ExitStack() as ctx:
        held = ctx.enter_context(tc.tile_pool(name="held", bufs=1))
        psum = ctx.enter_context(tc.psum_pool(name="psum", bufs=1))

        offsets = held.tile([P, S // 16], U16, name="offsets")
        word_table = held.tile([P, T], U16, name="word_table", align_bytes=64)
        scale_table = held.tile([P, T], U8, name="scale_table", align_bytes=64)
        w1_raw = [held.tile([P, 2, H], F32, name="w1_raw%d" % c, tag="w1_raw%d" % c, align_bytes=64) for c in range(2)]
        warm_in = held.tile([P, 1], F32, name="warm_in", tag="warm_then_gamma")
        warm_out = held.tile([P, 1], F32, name="warm_out")

        nc.gpsimd.memset(scale_table[:].bitcast(I32), 0)
        nc.gpsimd.memset(warm_in[:], 1.0)
        moments = held.tile([P, PACK, 2], F32, name="moments")
        nc.sync.dma_start(offsets[:], offs)
        nc.scalar.dma_start(out=word_table[:].bitcast(I32), in_=x_words[0].bitcast(I32))
        for q in range(4):
            (nc.sync if q < 2 else nc.scalar).dma_start(
                out=scale_table[32 * q : 32 * q + 4, :].bitcast(I32),
                in_=x_scales[0][4 * q : 4 * q + 4, :].bitcast(I32),
            )
        nc.scalar.activation(warm_out[:], warm_in[:], ACT.Abs_reciprocal_sqrt)
        w1_rows = w1.rearrange("(p j) c -> p j c", j=PACK)
        for c in range(2):
            nc.sync.dma_start(out=w1_raw[c][:], in_=w1_rows[:, 2 * c : 2 * c + 2, :])
        w2_raw = held.tile([P, PACK, N], F32, name="w2_raw", align_bytes=64)
        w2_dealt = w2.rearrange("(a t r) n -> r a t n", t=PACK, r=2)
        for r in range(2):
            nc.sync.dma_start(out=w2_raw[r:P:2], in_=w2_dealt[r])
        gam_run = held.tile([P, 2 * PACK - 1], F32, name="gam_run", tag="warm_then_gamma")
        gamma_rows = gamma.rearrange("(a e) o -> a (e o)", e=2 * PACK)
        for r in range(2):
            nc.scalar.dma_start(out=gam_run[r:P:2, :], in_=gamma_rows[:, r : r + 2 * PACK - 1])
        gam = gam_run[:, 0 : 2 * PACK - 1 : 2]

        x_codes = held.tile([P, S], U16, name="x_codes", align_bytes=64)
        x_sc = held.tile([P, S], U8, name="x_sc", align_bytes=64)
        nc.vector.tensor_copy(x_codes[:], word_table[:].indirect(offsets[:]))
        nc.vector.tensor_copy(x_sc[:], scale_table[:].indirect(offsets[:]))

        w1_bf = [held.tile([P, 2, P, PACK], BF16, name="w1_bf%d" % u, tag="w1_bf%d" % u, align_bytes=64) for u in range(2)]

        def cast_w1(engine_copy, c, lo, hi, first=0, last=P):
            src = w1_raw[c][:].rearrange("p j (a t r) -> p a j t r", t=PACK, r=2)[:, first // 2 : last // 2, :, lo:hi]
            dst = w1_bf[lo // 2][:, lo % 2 : lo % 2 + hi - lo, first:last, 2 * c : 2 * c + 2]
            engine_copy(dst.rearrange("p t (a r) j -> p a j t r", r=2), src)

        cast_w1(nc.scalar.copy, 0, 0, 2)
        cast_w1(nc.scalar.copy, 0, 2, 4, 0, SCALAR_CAST_COLS)
        cast_w1(nc.vector.tensor_copy, 0, 2, 4, SCALAR_CAST_COLS, P)
        cast_w1(nc.vector.tensor_copy, 1, 0, 1, 0, FIRST_CAST_COLS)
        cast_w1(nc.scalar.copy, 1, 0, 1, FIRST_CAST_COLS, P)
        cast_w1(nc.vector.tensor_copy, 1, 1, 2)
        cast_w1(nc.scalar.copy, 1, 2, 4, 0, LATE_CAST_COLS)
        cast_w1(nc.vector.tensor_copy, 1, 2, 4, LATE_CAST_COLS, P)

        w1_codes = held.tile([P, PACK, P], U32, name="w1_codes", align_bytes=64)
        w1_scales = held.tile([P, PACK, P], U8, name="w1_scales", align_bytes=64)
        for lo, hi in ((0, 1), (1, 2), (2, 4)):
            nc.vector.quantize_mx(
                out=w1_codes[:, lo:hi].rearrange("p t m -> p (t m)").bitcast(FP8X4),
                scales=w1_scales[:, lo:hi].rearrange("p t m -> p (t m)"),
                in_=w1_bf[lo // 2][:, lo % 2 : lo % 2 + hi - lo].rearrange("p t m j -> p (t m j)"),
            )

        h = []
        for t in range(PACK):
            banks = []
            for s in range(2):
                bank = psum.tile([P, HALF], F32, name="h%d_%d" % (t, s), tag="bank%d" % (2 * t + s))
                nc.tensor.matmul_mx(
                    out=bank[:],
                    lhsT=w1_codes[:, t, :].bitcast(FP8X4),
                    lhsT_scale=w1_scales[:, t, :],
                    rhs=x_codes[:, s * HALF : (s + 1) * HALF].bitcast(FP4X4),
                    rhs_scale=x_sc[:, s * HALF : (s + 1) * HALF],
                    start=True,
                    stop=True,
                )
                banks.append(bank)
            h.append(banks)

        neg_gam = held.tile([P, PACK], F32, name="neg_gam")
        nc.scalar.activation(neg_gam[:], gam, ACT.Copy, scale=-1.0)
        unscaled = held.tile([P, PACK, 2], F32, name="unscaled")
        nc.scalar.copy(unscaled[:, :, 0], gam)
        w2_bf = held.tile([P, N, PACK], BF16, name="w2_bf", tag="w1_bf1", align_bytes=64)
        nc.gpsimd.tensor_scalar(w2_bf[:], w2_raw[:].rearrange("p j n -> p n j"), 1.0, 0.0, ALU.mult, ALU.add)

        stats = [
            held.tile([P, 2, 6], F32, name="stats%d" % t, tag="stats%d" % t, align_bytes=64) for t in range(PACK)
        ]
        rstd = held.tile([P, PACK], F32, name="rstd")
        coef = [held.tile([P, 2], F32, name="coef%d" % t) for t in range(PACK)]
        early = [
            held.tile([P, 2, HALF], F32, name="early%d" % t, tag="early%d" % t, align_bytes=64) for t in range(PACK)
        ]
        normed = held.tile([P, PACK, 2, HALF], BF16, name="normed", align_bytes=64)
        w2q = []

        def stat(t, s):
            nc.vector.bn_stats(stats[t][:, s, :], h[t][s][:])

        def aggr(t):
            nc.vector.bn_aggr(moments[:, t, :], stats[t][:].rearrange("p s v -> p (s v)"))

        def inv_dev(t):
            nc.scalar.activation(rstd[:, t : t + 1], moments[:, t, 1:2], ACT.Abs_reciprocal_sqrt, bias=EPS)

        def shift(t):
            nc.scalar.activation(unscaled[:, t, 1:2], moments[:, t, 0:1], ACT.Copy, scale=neg_gam[:, t : t + 1])

        def scale_bias(t):
            nc.scalar.activation(coef[t][:], unscaled[:, t, :], ACT.Copy, scale=rstd[:, t : t + 1])

        def scale_only(t):
            nc.scalar.activation(coef[t][:, 0:1], unscaled[:, t, 0:1], ACT.Copy, scale=rstd[:, t : t + 1])

        def scale_vector(t):
            nc.vector.tensor_scalar_mul(coef[t][:, 0:1], rstd[:, t : t + 1], unscaled[:, t, 0:1])

        def copy_early(t, s, lo=0, hi=HALF):
            nc.scalar.activation(early[t][:, s, lo:hi], h[t][s][:, lo:hi], ACT.Copy, scale=gam_run[:, 2 * t : 2 * t + 1])

        def finish(engine, t, s, lo=0, hi=HALF):
            engine.tensor_scalar(
                normed[:, t, s, lo:hi], early[t][:, s, lo:hi], unscaled[:, t, 1:2], rstd[:, t : t + 1], ALU.add, ALU.mult
            )

        def finish_plane(engine, t):
            engine.tensor_scalar(
                normed[:, t], early[t][:], unscaled[:, t, 1:2], rstd[:, t : t + 1], ALU.add, ALU.mult
            )

        def finish_both(engine, t, lo, hi):
            engine.tensor_scalar(
                normed[:, t, :, lo:hi], early[t][:, :, lo:hi], unscaled[:, t, 1:2], rstd[:, t : t + 1], ALU.add, ALU.mult
            )

        def quantise_w2(tag, scale_tag):
            codes = held.tile([P, N], U32, name="w2_codes", tag=tag, align_bytes=64)
            scales = held.tile([P, N], U8, name="w2_scales", tag=scale_tag, align_bytes=64)
            nc.vector.quantize_mx(
                out=codes[:].bitcast(FP8X4), scales=scales[:], in_=w2_bf[:].rearrange("p n j -> p (n j)")
            )
            w2q.extend([codes, scales])

        def norm_scalar(t, s, lo=0, hi=HALF):
            nc.scalar.activation(
                normed[:, t, s, lo:hi], h[t][s][:, lo:hi], ACT.Identity, bias=coef[t][:, 1:2], scale=coef[t][:, 0:1]
            )

        def norm_vector(t, s, lo=0, hi=HALF):
            nc.vector.tensor_scalar(
                normed[:, t, s, lo:hi], h[t][s][:, lo:hi], moments[:, t, 0:1], coef[t][:, 0:1], ALU.subtract, ALU.mult
            )

        stat(0, 0)
        copy_early(0, 0)
        stat(0, 1)
        copy_early(0, 1)
        aggr(0)
        inv_dev(0)
        shift(0)
        finish_plane(nc.gpsimd, 0)
        stat(1, 0)
        stat(1, 1)
        copy_early(1, 1)
        aggr(1)
        inv_dev(1)
        shift(1)
        finish(nc.gpsimd, 1, 1)
        scale_only(1)
        stat(2, 0)
        copy_early(2, 0)
        stat(2, 1)
        copy_early(2, 1)
        aggr(2)
        inv_dev(2)
        shift(2)
        stat(3, 0)
        stat(3, 1)
        aggr(3)
        inv_dev(3)
        shift(3)
        scale_bias(3)
        copy_early(3, 0, 0, QUARTER)
        copy_early(3, 1, 0, QUARTER)
        norm_vector(1, 0)
        quantise_w2("early1", "w2s")
        finish_plane(nc.vector, 2)
        finish(nc.vector, 3, 0, 0, QUARTER)
        finish(nc.vector, 3, 1, 0, QUARTER)
        norm_vector(3, 0, QUARTER, HALF)
        norm_scalar(3, 1, QUARTER, HALF)
        w2_codes, w2_scales = w2q

        z_bf = held.tile([P, S, PACK], BF16, name="z_bf", align_bytes=64)
        z_codes = held.tile([P, S], U32, name="z_codes", align_bytes=64)
        z_scales = held.tile([P, S], U8, name="z_scales", align_bytes=64)
        result = held.tile([P, S], F32, name="result", align_bytes=64)
        planes = normed[:].rearrange("p t s n -> p t (s n)")

        def weave_views(lo, hi):
            dst = z_bf[:, lo:hi, :].rearrange("p (g i) t -> p g t i", i=4)
            return dst, planes[:, :, lo:hi].rearrange("p t (g i) -> p g t i", i=4)

        def weave_vector(lo, hi):
            dst, src = weave_views(lo, hi)
            nc.vector.tensor_scalar_max(dst, src, 0.0)

        def weave_scalar(lo, hi):
            dst, src = weave_views(lo, hi)
            nc.scalar.activation(dst, src, ACT.Relu)

        def quantise_z(lo, hi):
            nc.vector.quantize_mx(
                out=z_codes[:, lo:hi].bitcast(FP8X4),
                scales=z_scales[:, lo:hi],
                in_=z_bf[:, lo:hi, :].rearrange("p n t -> p (n t)"),
            )

        def second_layer(lo, hi, bank, engine_copy):
            acc = psum.tile([P, hi - lo], F32, name="acc%d" % bank, tag="bank%d" % bank)
            nc.tensor.matmul_mx(
                out=acc[:],
                lhsT=w2_codes[:].bitcast(FP8X4),
                lhsT_scale=w2_scales[:],
                rhs=z_codes[:, lo:hi].bitcast(FP8X4),
                rhs_scale=z_scales[:, lo:hi],
                start=True,
                stop=True,
            )
            engine_copy(result[:, lo:hi], acc[:])

        def store(lo, hi, queue):
            queue.dma_start(out=out[:, lo:hi], in_=result[:, lo:hi])

        weave_vector(0, 128)
        weave_vector(128, 256)
        weave_scalar(256, 384)
        weave_scalar(384, 448)
        quantise_z(0, 128)
        second_layer(0, 128, 0, nc.scalar.copy)
        store(0, 128, nc.sync)
        weave_vector(448, 512)
        quantise_z(128, 256)
        second_layer(128, 256, 1, nc.scalar.copy)
        store(128, 256, nc.sync)
        quantise_z(256, 384)
        second_layer(256, 384, 2, nc.scalar.copy)
        store(256, 384, nc.scalar)
        quantise_z(448, 512)
        second_layer(448, 512, 4, nc.scalar.copy)
        quantise_z(384, 448)
        second_layer(384, 448, 3, nc.vector.tensor_copy)
        store(384, 512, nc.sync)
